import numpy as np
import ml_dtypes


def mxq(x, axis, fmt="e4m3"):
    dtype, down = {"e4m3": (ml_dtypes.float8_e4m3fn, 7), "e5m2": (ml_dtypes.float8_e5m2, 14)}[fmt]
    v = np.moveaxis(np.asarray(x, np.float32).astype(ml_dtypes.bfloat16).astype(np.float64), axis, -1)
    blocks = v.reshape(v.shape[:-1] + (-1, 32))
    amax = np.abs(blocks).max(-1, keepdims=True)
    byte = np.maximum(np.where(amax > 0, np.frexp(amax)[1] - 1 + 127, 0) - down, 1)
    scale = np.exp2(byte - 127.0)
    codes = (blocks / scale).astype(np.float32).astype(dtype).astype(np.float64)
    return np.moveaxis((codes * scale).reshape(v.shape), -1, axis)


WIDE = False


def mx_kscale(k):
    if not WIDE:
        return np.ones(k)
    levels = np.array([10, -10, 5, -5, 0])
    if k % 512:
        return np.exp2(np.random.permutation(np.resize(levels, k // 32))).repeat(32)
    a = np.empty((k // 512, 16))
    for p in range(k // 512):
        a[p, :8] = np.random.permutation(np.resize(levels, 8))
        for g in range(8):
            far = levels[np.abs(levels - a[p, g]) >= 10]
            a[p, g + 8] = far[np.random.randint(len(far))]
    return np.exp2(a.ravel()).repeat(32)


def f64(x):
    return np.asarray(x).astype(np.float64)


def striped(idx):
    return np.tile(idx.reshape(-1, 16).T, (8, 1)).astype(np.uint16)


def unstriped(offs):
    return offs[:16].T.reshape(-1).astype(np.int64)


def pack_weight(w):
    k, n = w.shape
    w = f64(np.asarray(w, np.float32).astype(ml_dtypes.bfloat16)).reshape(k // 32, 32, n)
    amax = np.abs(w).max(1)
    byte = np.clip(np.where(amax > 0, np.frexp(amax)[1] - 1 + 127 - 7, 1), 1, 254)
    scaled = (w * np.exp2(127.0 - byte)[:, None, :]).reshape(k, n).astype(np.float32)
    words = np.ascontiguousarray(scaled.reshape(k // 512, 128, 4, n).transpose(0, 1, 3, 2)).astype(ml_dtypes.float8_e4m3fn).view(np.uint8)
    return words, np.ascontiguousarray(byte.astype(np.uint8).reshape(k // 512, 16, n))


def unpack_weight(words, scales):
    g, p, n, _ = words.shape
    vals = np.ascontiguousarray(words).view(ml_dtypes.float8_e4m3fn).astype(np.float64) * np.repeat(np.exp2(scales.astype(np.float64) - 127.0), 8, axis=1)[..., None]
    return vals.transpose(0, 1, 3, 2).reshape(g * 512, n)


def relu(v):
    return np.maximum(v, 0.0)


K, T, S, V, H, N = 1024, 2048, 512, 256, 512, 128


def setup_inputs():
    n = np.random.standard_normal
    s = mx_kscale(K)[:, None]
    u = mx_kscale(H)
    near = np.random.permutation(S)
    packed_xT = pack_weight(n((K, T)) * s)
    return {
        "x_words": packed_xT[0],
        "x_scales": packed_xT[1],
        "w1": (n((K, H)) / np.sqrt(K) / s * u).astype(np.float32),
        "w2": (n((K, H)) / np.sqrt(K) / s * u).astype(np.float32),
        "w3": (n((H, N)) / np.sqrt(H) / u[:, None]).astype(np.float32),
        "offs": striped(np.random.permutation(T)[:S]),
        "pos1": striped(near[:V]),
        "pos2": striped(near[V:]),
        "pos3": striped(np.random.permutation(S)[:V]),
    }


def reference(x_words, x_scales, w1, w2, w3, offs, pos1, pos2, pos3):
    xq = unpack_weight(x_words, x_scales)[:, unstriped(offs)]
    a = mxq(f64(w1), 0, "e4m3").T @ xq
    a0 = a[:, unstriped(pos1)]
    y = mxq(f64(w2), 0, "e4m3").T @ xq
    y1 = y[:, unstriped(pos2)]
    y2 = y[:, unstriped(pos3)]
    a1 = a[:, unstriped(pos2)]
    z = relu(a0 + y1) + relu(a0 + y2) + relu(a1 + y2)
    return relu(mxq(f64(w3), 0, "e4m3").T @ mxq(z, 0, "e4m3"))

@@ -1,0 +1,216 @@
+from contextlib import ExitStack
+
+import concourse.mybir as mybir
+from concourse.masks import make_identity
+
+K, T, S, V, H, N = 1024, 2048, 512, 256, 512, 128
+FLOPS = 2 * (2 * K * H * S + H * N * V)
+
+F32 = mybir.dt.float32
+BF16 = mybir.dt.bfloat16
+I32 = mybir.dt.int32
+U32 = mybir.dt.uint32
+U16 = mybir.dt.uint16
+U8 = mybir.dt.uint8
+FP8X4 = mybir.dt.float8_e4m3fn_x4
+ALU = mybir.AluOpType
+ACT = mybir.ActivationFunctionType
+
+P = 128
+PACK = 4
+K_PASS = P * PACK
+PASSES = K // K_PASS
+TILES = H // P
+HALVES = V // P
+BANK = 512
+QUADRANT = 32
+RUN = 4
+
+
+def tile_picked_yjano_relu_p_kernel(
+    tc, x_words, x_scales, w1, w2, w3, offs, pos1, pos2, pos3, out
+):
+    nc = tc.nc
+    with ExitStack() as ctx:
+        keep = ctx.enter_context(tc.tile_pool(name="keep", bufs=1))
+        ring = ctx.enter_context(tc.tile_pool(name="ring", bufs=2))
+        psum = ctx.enter_context(tc.psum_pool(name="psum", bufs=1))
+
+        def load_list(name, source):
+            offsets = keep.tile(list(source.shape), U16, name=name)
+            nc.sync.dma_start(offsets[:], source)
+            return offsets
+
+        def load_words(o):
+            table = keep.tile([P, T], U32, name="words%d" % o)
+            nc.sync.dma_start(
+                table[:].bitcast(I32),
+                x_words[o].rearrange("p n t -> p (n t)").bitcast(I32),
+            )
+            return table
+
+        def load_rows(name, w, o, cols):
+            raw = keep.tile([P, PACK, P], F32, name=name, tag=name)
+            rows = w[o * K_PASS : (o + 1) * K_PASS, cols]
+            nc.sync.dma_start(raw[:], rows.rearrange("(p j) c -> p j c", j=PACK))
+            return raw
+
+        def load_piece(m, j, o):
+            w = (w1, w2)[m]
+            return load_rows("raw%d_%d" % (2 * j + m, o), w, o, slice(j * P, (j + 1) * P))
+
+        scale_table = keep.tile([P, T], U8, name="scale_table")
+        nc.gpsimd.memset(scale_table[:].bitcast(I32), 0)
+        for q in range(P // QUADRANT):
+            (nc.scalar, nc.gpsimd)[q // 2].dma_start(
+                scale_table[QUADRANT * q : QUADRANT * q + 4 * PASSES, :].bitcast(I32),
+                x_scales[:, 4 * q : 4 * q + 4, :].bitcast(I32),
+            )
+
+        raw = {}
+        picked = load_list("picked", offs)
+        words0 = load_words(0)
+        raw[0, 0, 0] = load_piece(0, 0, 0)
+        raw[0, 0, 1] = load_piece(0, 0, 1)
+        words1 = load_words(1)
+        for o in range(PASSES):
+            raw[1, 0, o] = load_piece(1, 0, o)
+        first = load_list("first", pos1)
+        second = load_list("second", pos2)
+        third = load_list("third", pos3)
+        for j in range(1, TILES):
+            for m in range(2):
+                for o in range(PASSES):
+                    raw[m, j, o] = load_piece(m, j, o)
+        raw3 = load_rows("raw3", w3, 0, slice(0, N))
+
+        ident = keep.tile([P, P], F32, name="ident")
+        make_identity(nc, ident[:])
+
+        def interleave(grouped, rows, on_vector=False):
+            target = grouped.rearrange("p (c i) j -> p c j i", i=RUN)
+            source = rows[:].rearrange("p j (c i) -> p c j i", i=RUN)
+            if on_vector:
+                nc.vector.tensor_copy(target, source)
+            else:
+                nc.scalar.activation(target, source, ACT.Copy)
+
+        def bank(tag, bufs=1):
+            return psum.tile([P, BANK], F32, name=tag, bufs=bufs)
+
+        def quantise(name, grouped, width):
+            codes = keep.tile([P, width], U32, name=name + "_codes", align_bytes=64)
+            scales = keep.tile([P, width], U8, name=name + "_scales", align_bytes=64)
+            nc.vector.quantize_mx(codes[:].bitcast(FP8X4), scales[:], grouped)
+            return codes, scales
+
+        def prepare(m, j):
+            grouped = keep.tile([P, PASSES * P, PACK], BF16, name="grouped%d_%d" % (m, j), align_bytes=64)
+            for o in range(PASSES):
+                interleave(grouped[:, o * P : (o + 1) * P, :], raw[m, j, o], (m, j, o) in ((1, 0, 1), (0, 1, 0)))
+            return quantise("w%d_%d" % (m, j), grouped[:].rearrange("p c j -> p (c j)"), PASSES * P)
+
+        x_codes = [keep.tile([P, S], U32, name="x_codes%d" % o, align_bytes=64) for o in range(PASSES)]
+        x_planes = keep.tile([P, S], U8, name="x_planes", align_bytes=64)
+
+        def project(m, j, weights):
+            codes, scales = weights
+            acc = bank("acc", 4)
+            for o in range(PASSES):
+                cols = slice(o * P, (o + 1) * P)
+                nc.tensor.matmul_mx(
+                    out=acc[:],
+                    lhsT=codes[:, cols].bitcast(FP8X4),
+                    lhsT_scale=scales[:, cols],
+                    rhs=x_codes[o][:].bitcast(FP8X4),
+                    rhs_scale=x_planes[4 * o :, :],
+                    start=(o == 0),
+                    stop=(o == PASSES - 1),
+                )
+            rows = keep.tile([P, S], F32, name="rows%d_%d" % (m, j), tag="raw%d_0" % (2 * j + m + 2 if 2 * j + m >= 1 else -1 - 2 * j - m))
+            nc.scalar.copy(rows[:], acc[:])
+            return rows
+
+        def fetch(rows, offsets, name):
+            got = keep.tile([P, V], F32, name=name)
+            nc.vector.tensor_copy(got[:], rows[:].indirect(offsets[:]))
+            return got
+
+        def turn(target, source, start=False, stop=False):
+            for h in range(HALVES):
+                cols = slice(h * P, (h + 1) * P)
+                nc.tensor.matmul(
+                    target[:, cols],
+                    source[:, cols],
+                    ident[:],
+                    start=start and h == 0,
+                    stop=stop and h == HALVES - 1,
+                    is_transpose=True,
+                )
+
+        z_turned = [keep.tile([P, H], BF16, name="z_turned%d" % h) for h in range(HALVES)]
+
+        def sum_pairs(j, early, late):
+            one = keep.tile([P, V], F32, name="one%d" % j, tag="raw%d_1" % (2 * j + 5))
+            nc.scalar.activation(one[:], early[:, 0:V], ACT.Relu)
+            two = ring.tile([P, V], F32, name="two")
+            nc.vector.scalar_tensor_tensor(two[:], early[:, V : 2 * V], 0.0, one[:], ALU.max, ALU.add)
+            for h in range(HALVES):
+                cols = slice(h * P, (h + 1) * P)
+                nc.vector.scalar_tensor_tensor(
+                    z_turned[h][:, j * P : (j + 1) * P], late[:, cols], 0.0, two[:, cols], ALU.max, ALU.add
+                )
+
+        nc.vector.tensor_copy(x_planes[:], scale_table[:].indirect(picked[:]))
+        nc.vector.tensor_copy(x_codes[0][:], words0[:].indirect(picked[:]))
+        weights_a = prepare(0, 0)
+        nc.vector.tensor_copy(x_codes[1][:], words1[:].indirect(picked[:]))
+        a = project(0, 0, weights_a)
+        y = project(1, 0, prepare(1, 0))
+
+        for j in range(TILES):
+            a0 = fetch(a, first, "a0_%d" % j)
+            a1 = fetch(a, second, "a1_%d" % j)
+            if j + 1 < TILES:
+                a = project(0, j + 1, prepare(0, j + 1))
+            early = bank("early", 2)
+            late = bank("late", 2)
+            turn(early[:, 0:V], a0, start=True)
+            turn(early[:, V : 2 * V], a1)
+            turn(late[:, 0:V], a0, start=True)
+            y2 = fetch(y, third, "y2_%d" % j)
+            y1 = fetch(y, second, "y1_%d" % j)
+            if j + 1 < TILES:
+                y = project(1, j + 1, prepare(1, j + 1))
+            turn(early[:, 0:V], y2)
+            turn(early[:, V : 2 * V], y2, stop=True)
+            turn(late[:, 0:V], y1, stop=True)
+            sum_pairs(j, early, late)
+
+        grouped3 = keep.tile([P, N, PACK], BF16, name="grouped3", align_bytes=64)
+        interleave(grouped3[:], raw3)
+        w3_codes, w3_scales = quantise("w3", grouped3[:].rearrange("p c j -> p (c j)"), N)
+
+        for h in range(HALVES):
+            pairs = z_turned[h][:].bitcast(F32)
+            back = bank("acc", 4)
+            for u in range(2):
+                nc.tensor.transpose(back[:, u * P : (u + 1) * P], pairs[:, u : H // 2 : 2], ident[:])
+            z_grouped = keep.tile([P, P, 2], F32, name="z_grouped%d" % h, align_bytes=64)
+            nc.scalar.copy(z_grouped[:], back[:, 0 : 2 * P].rearrange("p (u v) -> p v u", u=2))
+            z_codes, z_scales = quantise(
+                "z%d" % h, z_grouped[:].rearrange("p v u -> p (v u)").bitcast(BF16), P
+            )
+            acc = bank("acc", 4)
+            nc.tensor.matmul_mx(
+                out=acc[:, 0:P],
+                lhsT=w3_codes[:].bitcast(FP8X4),
+                lhsT_scale=w3_scales[:],
+                rhs=z_codes[:].bitcast(FP8X4),
+                rhs_scale=z_scales[:],
+                start=True,
+                stop=True,
+            )
+            result = keep.tile([P, P], F32, name="result%d" % h)
+            nc.scalar.activation(result[:], acc[:, 0:P], ACT.Relu)
+            nc.sync.dma_start(out[:, h * P : (h + 1) * P], result[:])

@@ -42,7 +42,7 @@ def tile_picked_yjano_relu_p_kernel(
             return offsets
 
         def load_words(o):
-            table = keep.tile([P, T], U32, name="words%d" % o)
+            table = keep.tile([P, T], U32, name="words%d" % o, tag="words%d" % o, align_bytes=64)
             nc.sync.dma_start(
                 table[:].bitcast(I32),
                 x_words[o].rearrange("p n t -> p (n t)").bitcast(I32),
@@ -50,7 +50,7 @@ def tile_picked_yjano_relu_p_kernel(
             return table
 
         def load_rows(name, w, o, cols):
-            raw = keep.tile([P, PACK, P], F32, name=name, tag=name)
+            raw = keep.tile([P, PACK, P], F32, name=name, tag=name, align_bytes=64)
             rows = w[o * K_PASS : (o + 1) * K_PASS, cols]
             nc.sync.dma_start(raw[:], rows.rearrange("(p j) c -> p j c", j=PACK))
             return raw
@@ -61,15 +61,15 @@ def tile_picked_yjano_relu_p_kernel(
 
         scale_table = keep.tile([P, T], U8, name="scale_table")
         nc.gpsimd.memset(scale_table[:].bitcast(I32), 0)
-        for q in range(P // QUADRANT):
-            (nc.scalar, nc.gpsimd)[q // 2].dma_start(
-                scale_table[QUADRANT * q : QUADRANT * q + 4 * PASSES, :].bitcast(I32),
-                x_scales[:, 4 * q : 4 * q + 4, :].bitcast(I32),
-            )
 
         raw = {}
         picked = load_list("picked", offs)
         words0 = load_words(0)
+        for q in range(P // QUADRANT):
+            nc.sync.dma_start(
+                scale_table[QUADRANT * q : QUADRANT * q + 4 * PASSES, :].bitcast(I32),
+                x_scales[:, 4 * q : 4 * q + 4, :].bitcast(I32),
+            )
         raw[0, 0, 0] = load_piece(0, 0, 0)
         raw[0, 0, 1] = load_piece(0, 0, 1)
         words1 = load_words(1)
@@ -99,7 +99,7 @@ def tile_picked_yjano_relu_p_kernel(
             return psum.tile([P, BANK], F32, name=tag, bufs=bufs)
 
         def quantise(name, grouped, width):
-            codes = keep.tile([P, width], U32, name=name + "_codes", align_bytes=64)
+            codes = keep.tile([P, width], U32, name=name + "_codes", tag={"w1_0": "words1", "w3": "raw11_1"}.get(name, name), align_bytes=64)
             scales = keep.tile([P, width], U8, name=name + "_scales", align_bytes=64)
             nc.vector.quantize_mx(codes[:].bitcast(FP8X4), scales[:], grouped)
             return codes, scales
@@ -107,7 +107,7 @@ def tile_picked_yjano_relu_p_kernel(
         def prepare(m, j):
             grouped = keep.tile([P, PASSES * P, PACK], BF16, name="grouped%d_%d" % (m, j), align_bytes=64)
             for o in range(PASSES):
-                interleave(grouped[:, o * P : (o + 1) * P, :], raw[m, j, o], (m, j, o) in ((1, 0, 1), (0, 1, 0)))
+                interleave(grouped[:, o * P : (o + 1) * P, :], raw[m, j, o], (m, j, o) in ((0, 1, 0), (0, 1, 1)))
             return quantise("w%d_%d" % (m, j), grouped[:].rearrange("p c j -> p (c j)"), PASSES * P)
 
         x_codes = [keep.tile([P, S], U32, name="x_codes%d" % o, align_bytes=64) for o in range(PASSES)]
@@ -127,7 +127,7 @@ def tile_picked_yjano_relu_p_kernel(
                     start=(o == 0),
                     stop=(o == PASSES - 1),
                 )
-            rows = keep.tile([P, S], F32, name="rows%d_%d" % (m, j), tag="raw%d_0" % (2 * j + m + 2 if 2 * j + m >= 1 else -1 - 2 * j - m))
+            rows = keep.tile([P, S], F32, name="rows%d_%d" % (m, j), tag="raw%d_0" % (2 * j + m + 2 if 2 * j + m >= 0 else -1 - 2 * j - m), align_bytes=64)
             nc.scalar.copy(rows[:], acc[:])
             return rows
 
@@ -151,18 +151,25 @@ def tile_picked_yjano_relu_p_kernel(
         z_turned = [keep.tile([P, H], BF16, name="z_turned%d" % h) for h in range(HALVES)]
 
         def sum_pairs(j, early, late):
-            one = keep.tile([P, V], F32, name="one%d" % j, tag="raw%d_1" % (2 * j + 5))
+            one = keep.tile([P, V], F32, name="one%d" % j, tag="raw%d_1" % (2 * j + 5), align_bytes=64)
             nc.scalar.activation(one[:], early[:, 0:V], ACT.Relu)
             two = ring.tile([P, V], F32, name="two")
-            nc.vector.scalar_tensor_tensor(two[:], early[:, V : 2 * V], 0.0, one[:], ALU.max, ALU.add)
+            for h in range(HALVES):
+                cols = slice(h * P, (h + 1) * P)
+                nc.vector.scalar_tensor_tensor(two[:, cols], late[:, cols], 0.0, one[:, cols], ALU.max, ALU.add)
             for h in range(HALVES):
                 cols = slice(h * P, (h + 1) * P)
                 nc.vector.scalar_tensor_tensor(
-                    z_turned[h][:, j * P : (j + 1) * P], late[:, cols], 0.0, two[:, cols], ALU.max, ALU.add
+                    z_turned[h][:, j * P : (j + 1) * P],
+                    late[:, V + h * P : V + (h + 1) * P],
+                    0.0,
+                    two[:, cols],
+                    ALU.max,
+                    ALU.add,
                 )
 
-        nc.vector.tensor_copy(x_planes[:], scale_table[:].indirect(picked[:]))
         nc.vector.tensor_copy(x_codes[0][:], words0[:].indirect(picked[:]))
+        nc.vector.tensor_copy(x_planes[:], scale_table[:].indirect(picked[:]))
         weights_a = prepare(0, 0)
         nc.vector.tensor_copy(x_codes[1][:], words1[:].indirect(picked[:]))
         a = project(0, 0, weights_a)
@@ -176,15 +183,15 @@ def tile_picked_yjano_relu_p_kernel(
             early = bank("early", 2)
             late = bank("late", 2)
             turn(early[:, 0:V], a0, start=True)
-            turn(early[:, V : 2 * V], a1)
-            turn(late[:, 0:V], a0, start=True)
+            turn(late[:, V : 2 * V], a0, start=True)
+            turn(late[:, 0:V], a1)
             y2 = fetch(y, third, "y2_%d" % j)
             y1 = fetch(y, second, "y1_%d" % j)
             if j + 1 < TILES:
                 y = project(1, j + 1, prepare(1, j + 1))
-            turn(early[:, 0:V], y2)
-            turn(early[:, V : 2 * V], y2, stop=True)
-            turn(late[:, 0:V], y1, stop=True)
+            turn(early[:, 0:V], y2, stop=True)
+            turn(late[:, 0:V], y2)
+            turn(late[:, V : 2 * V], y1, stop=True)
             sum_pairs(j, early, late)
 
         grouped3 = keep.tile([P, N, PACK], BF16, name="grouped3", align_bytes=64)
@@ -197,7 +204,8 @@ def tile_picked_yjano_relu_p_kernel(
             for u in range(2):
                 nc.tensor.transpose(back[:, u * P : (u + 1) * P], pairs[:, u : H // 2 : 2], ident[:])
             z_grouped = keep.tile([P, P, 2], F32, name="z_grouped%d" % h, align_bytes=64)
-            nc.scalar.copy(z_grouped[:], back[:, 0 : 2 * P].rearrange("p (u v) -> p v u", u=2))
+            move = (nc.scalar.copy, nc.vector.tensor_copy)[h]
+            move(z_grouped[:], back[:, 0 : 2 * P].rearrange("p (u v) -> p v u", u=2))
             z_codes, z_scales = quantise(
                 "z%d" % h, z_grouped[:].rearrange("p v u -> p (v u)").bitcast(BF16), P
             )
@@ -212,5 +220,8 @@ def tile_picked_yjano_relu_p_kernel(
                 stop=True,
             )
             result = keep.tile([P, P], F32, name="result%d" % h)
-            nc.scalar.activation(result[:], acc[:, 0:P], ACT.Relu)
+            if h == 0:
+                nc.scalar.activation(result[:], acc[:, 0:P], ACT.Relu)
+            else:
+                nc.vector.tensor_scalar(result[:], acc[:, 0:P], 0.0, None, ALU.max)
             nc.sync.dma_start(out[:, h * P : (h + 1) * P], result[:])

@@ -21,10 +21,16 @@ PACK = 4
 K_PASS = P * PACK
 PASSES = K // K_PASS
 TILES = H // P
+PIECES = 2 * TILES
+PARTS = PASSES * PIECES
 HALVES = V // P
 BANK = 512
 QUADRANT = 32
+STRIPE = 16
 RUN = 4
+ACC_BANKS = 4
+HEAD_PARTS = 5
+VECTOR_PARTS = (3,)
 
 
 def tile_picked_yjano_relu_p_kernel(
@@ -42,93 +48,108 @@ def tile_picked_yjano_relu_p_kernel(
             return offsets
 
         def load_words(o):
-            table = keep.tile([P, T], U32, name="words%d" % o, tag="words%d" % o, align_bytes=64)
+            table = keep.tile([P, T], U32, name="words%d" % o, align_bytes=64)
             nc.sync.dma_start(
                 table[:].bitcast(I32),
                 x_words[o].rearrange("p n t -> p (n t)").bitcast(I32),
             )
             return table
 
-        def load_rows(name, w, o, cols):
-            raw = keep.tile([P, PACK, P], F32, name=name, tag=name, align_bytes=64)
-            rows = w[o * K_PASS : (o + 1) * K_PASS, cols]
-            nc.sync.dma_start(raw[:], rows.rearrange("(p j) c -> p j c", j=PACK))
-            return raw
+        def load_part(i):
+            n, o = divmod(i, PASSES)
+            j, m = divmod(n, 2)
+            source = (w1, w2)[m][o * K_PASS : (o + 1) * K_PASS, j * P : (j + 1) * P]
+            rows = keep.tile([P, PACK, P], F32, name="raw%d" % i, align_bytes=64)
+            nc.sync.dma_start(rows[:], source.rearrange("(p j) c -> p j c", j=PACK))
+            return rows
 
-        def load_piece(m, j, o):
-            w = (w1, w2)[m]
-            return load_rows("raw%d_%d" % (2 * j + m, o), w, o, slice(j * P, (j + 1) * P))
+        def load_last():
+            rows = keep.tile([P, PACK, N], F32, name="raw%d" % PARTS, align_bytes=64)
+            dealt = w3.rearrange("(b u r e) c -> u b r (e c)", u=2, r=8, e=2)
+            for u in range(2):
+                nc.sync.dma_start(rows[:, 2 * u : 2 * u + 2, :].rearrange("p e c -> p (e c)"), dealt[u])
+            return rows
 
-        scale_table = keep.tile([P, T], U8, name="scale_table")
+        scale_table = keep.tile([P, T], U8, name="scale_table", align_bytes=64)
         nc.gpsimd.memset(scale_table[:].bitcast(I32), 0)
 
-        raw = {}
-        picked = load_list("picked", offs)
         words0 = load_words(0)
+        picked = load_list("picked", offs)
         for q in range(P // QUADRANT):
             nc.sync.dma_start(
                 scale_table[QUADRANT * q : QUADRANT * q + 4 * PASSES, :].bitcast(I32),
                 x_scales[:, 4 * q : 4 * q + 4, :].bitcast(I32),
             )
-        raw[0, 0, 0] = load_piece(0, 0, 0)
-        raw[0, 0, 1] = load_piece(0, 0, 1)
+        raw = [load_part(i) for i in range(PASSES)]
         words1 = load_words(1)
-        for o in range(PASSES):
-            raw[1, 0, o] = load_piece(1, 0, o)
+        raw.extend(load_part(i) for i in range(PASSES, 2 * PASSES))
         first = load_list("first", pos1)
         second = load_list("second", pos2)
         third = load_list("third", pos3)
-        for j in range(1, TILES):
-            for m in range(2):
-                for o in range(PASSES):
-                    raw[m, j, o] = load_piece(m, j, o)
-        raw3 = load_rows("raw3", w3, 0, slice(0, N))
+        raw.extend(load_part(i) for i in range(2 * PASSES, PARTS))
+        raw.append(load_last())
 
         ident = keep.tile([P, P], F32, name="ident")
         make_identity(nc, ident[:])
 
-        def interleave(grouped, rows, on_vector=False):
-            target = grouped.rearrange("p (c i) j -> p c j i", i=RUN)
-            source = rows[:].rearrange("p j (c i) -> p c j i", i=RUN)
-            if on_vector:
+        def bank(tag):
+            return psum.tile([P, BANK], F32, name=tag)
+
+        def acc_bank(n):
+            return bank("acc%d" % (n % ACC_BANKS))
+
+        def cast(i):
+            grouped = ring.tile([P, P, PACK], BF16, name="grouped", bufs=4, align_bytes=64)
+            target = grouped[:].rearrange("p (c i) j -> p c j i", i=RUN)
+            source = raw[i][:].rearrange("p j (c i) -> p c j i", i=RUN)
+            if i in VECTOR_PARTS:
                 nc.vector.tensor_copy(target, source)
             else:
                 nc.scalar.activation(target, source, ACT.Copy)
-
-        def bank(tag, bufs=1):
-            return psum.tile([P, BANK], F32, name=tag, bufs=bufs)
+            return grouped[:].rearrange("p c j -> p (c j)")
 
         def quantise(name, grouped, width):
-            codes = keep.tile([P, width], U32, name=name + "_codes", tag={"w1_0": "words1", "w3": "raw11_1"}.get(name, name), align_bytes=64)
+            codes = keep.tile([P, width], U32, name=name + "_codes", align_bytes=64)
             scales = keep.tile([P, width], U8, name=name + "_scales", align_bytes=64)
             nc.vector.quantize_mx(codes[:].bitcast(FP8X4), scales[:], grouped)
             return codes, scales
 
-        def prepare(m, j):
-            grouped = keep.tile([P, PASSES * P, PACK], BF16, name="grouped%d_%d" % (m, j), align_bytes=64)
-            for o in range(PASSES):
-                interleave(grouped[:, o * P : (o + 1) * P, :], raw[m, j, o], (m, j, o) in ((0, 1, 0), (0, 1, 1)))
-            return quantise("w%d_%d" % (m, j), grouped[:].rearrange("p c j -> p (c j)"), PASSES * P)
+        weights = {}
 
-        x_codes = [keep.tile([P, S], U32, name="x_codes%d" % o, align_bytes=64) for o in range(PASSES)]
+        def quantise_part(i, grouped):
+            codes, scales = quantise("w%d" % i, grouped, P)
+            weights[i] = (codes[:].bitcast(FP8X4), scales[:])
+
+        x_codes = [keep.tile([P, S], U32, name="x_codes0", align_bytes=64)]
         x_planes = keep.tile([P, S], U8, name="x_planes", align_bytes=64)
+        accs = {}
 
-        def project(m, j, weights):
-            codes, scales = weights
-            acc = bank("acc", 4)
-            for o in range(PASSES):
-                cols = slice(o * P, (o + 1) * P)
-                nc.tensor.matmul_mx(
-                    out=acc[:],
-                    lhsT=codes[:, cols].bitcast(FP8X4),
-                    lhsT_scale=scales[:, cols],
-                    rhs=x_codes[o][:].bitcast(FP8X4),
-                    rhs_scale=x_planes[4 * o :, :],
-                    start=(o == 0),
-                    stop=(o == PASSES - 1),
-                )
-            rows = keep.tile([P, S], F32, name="rows%d_%d" % (m, j), tag="raw%d_0" % (2 * j + m + 2 if 2 * j + m >= 0 else -1 - 2 * j - m), align_bytes=64)
-            nc.scalar.copy(rows[:], acc[:])
+        def multiply(i, acc, cols):
+            o = i % PASSES
+            nc.tensor.matmul_mx(
+                out=acc[:, cols],
+                lhsT=weights[i][0],
+                lhsT_scale=weights[i][1],
+                rhs=x_codes[o][:, cols].bitcast(FP8X4),
+                rhs_scale=x_planes[4 * o :, cols],
+                start=(o == 0),
+                stop=(o == PASSES - 1),
+            )
+
+        def project(i, grouped):
+            quantise_part(i, grouped)
+            if i < PARTS:
+                n = i // PASSES
+                if n not in accs:
+                    accs[n] = acc_bank(n)
+                multiply(i, accs[n], slice(0, S))
+
+        def rows_tile():
+            return ring.tile([P, S], F32, name="rows", align_bytes=64)
+
+        def bring(n):
+            rows = rows_tile()
+            nc.scalar.copy(rows[:], accs[n][:])
             return rows
 
         def fetch(rows, offsets, name):
@@ -136,92 +157,159 @@ def tile_picked_yjano_relu_p_kernel(
             nc.vector.tensor_copy(got[:], rows[:].indirect(offsets[:]))
             return got
 
+        def fetch_half(got, rows, offsets, h):
+            entries = offsets[:, h * P // STRIPE : (h + 1) * P // STRIPE]
+            nc.vector.tensor_copy(got, rows[:].indirect(entries))
+
+        def turn_block(target, source, start=False, stop=False):
+            nc.tensor.matmul(target, source, ident[:], start=start, stop=stop, is_transpose=True)
+
         def turn(target, source, start=False, stop=False):
             for h in range(HALVES):
                 cols = slice(h * P, (h + 1) * P)
-                nc.tensor.matmul(
-                    target[:, cols],
-                    source[:, cols],
-                    ident[:],
-                    start=start and h == 0,
-                    stop=stop and h == HALVES - 1,
-                    is_transpose=True,
-                )
+                turn_block(target[:, cols], source[:, cols], start and h == 0, stop and h == HALVES - 1)
 
-        z_turned = [keep.tile([P, H], BF16, name="z_turned%d" % h) for h in range(HALVES)]
+        def turn_pair(target, left, right):
+            turn(target, left, start=True)
+            turn(target, right, stop=True)
 
-        def sum_pairs(j, early, late):
-            one = keep.tile([P, V], F32, name="one%d" % j, tag="raw%d_1" % (2 * j + 5), align_bytes=64)
-            nc.scalar.activation(one[:], early[:, 0:V], ACT.Relu)
+        z_turned = keep.tile([P, HALVES, 2, H // 2], BF16, name="z_turned")
+
+        def relu_add(target, sums, other):
+            nc.vector.scalar_tensor_tensor(target, sums, 0.0, other, ALU.max, ALU.add)
+
+        def open_sums(both):
+            one = ring.tile([P, V], F32, name="one")
+            nc.scalar.activation(one[:], both[0], ACT.Relu)
+            return one
+
+        def join_sums(both, one):
             two = ring.tile([P, V], F32, name="two")
-            for h in range(HALVES):
-                cols = slice(h * P, (h + 1) * P)
-                nc.vector.scalar_tensor_tensor(two[:, cols], late[:, cols], 0.0, one[:, cols], ALU.max, ALU.add)
-            for h in range(HALVES):
-                cols = slice(h * P, (h + 1) * P)
-                nc.vector.scalar_tensor_tensor(
-                    z_turned[h][:, j * P : (j + 1) * P],
-                    late[:, V + h * P : V + (h + 1) * P],
-                    0.0,
-                    two[:, cols],
-                    ALU.max,
-                    ALU.add,
-                )
+            relu_add(two[:], both[1], one[:])
+            return two
+
+        def by_word(columns, u):
+            return columns.rearrange("p (h g u w) -> p u h g w", g=4, u=2, w=16)[:, u]
+
+        def close_sums(j, first_half, last, two):
+            halves = last.shape[1] // P
+            for u in range(2):
+                target = z_turned[:, first_half : first_half + halves, u, j * P // 2 : (j + 1) * P // 2]
+                relu_add(target.rearrange("p h (g w) -> p h g w", w=16), by_word(last, u), by_word(two, u))
 
         nc.vector.tensor_copy(x_codes[0][:], words0[:].indirect(picked[:]))
         nc.vector.tensor_copy(x_planes[:], scale_table[:].indirect(picked[:]))
-        weights_a = prepare(0, 0)
-        nc.vector.tensor_copy(x_codes[1][:], words1[:].indirect(picked[:]))
-        a = project(0, 0, weights_a)
-        y = project(1, 0, prepare(1, 0))
+        x_codes.append(keep.tile([P, S], U32, name="x_codes1", align_bytes=64))
+        for i in range(PASSES):
+            quantise_part(i, cast(i))
+        half_banks = (acc_bank(0), bank("spare0"))
+        a = rows_tile()
+        for h in range(2):
+            cols = slice(h * S // 2, (h + 1) * S // 2)
+            entries = picked[:, cols.start // STRIPE : cols.stop // STRIPE]
+            nc.vector.tensor_copy(x_codes[1][:, cols], words1[:].indirect(entries))
+            for i in range(PASSES):
+                multiply(i, half_banks[h], cols)
+            nc.scalar.copy(a[:, cols], half_banks[h][:, cols])
+        for i in range(PASSES, HEAD_PARTS):
+            project(i, cast(i))
 
+        before = None
         for j in range(TILES):
+            n = 2 * j
+            part = HEAD_PARTS + PASSES * n
+            final = j == TILES - 1
+            if before:
+                a = bring(n)
+            if not final:
+                early = cast(part)
+            if before:
+                one = open_sums(before[0])
+            if not final:
+                late = cast(part + 1)
             a0 = fetch(a, first, "a0_%d" % j)
+            if final:
+                break
             a1 = fetch(a, second, "a1_%d" % j)
-            if j + 1 < TILES:
-                a = project(0, j + 1, prepare(0, j + 1))
-            early = bank("early", 2)
-            late = bank("late", 2)
-            turn(early[:, 0:V], a0, start=True)
-            turn(late[:, V : 2 * V], a0, start=True)
-            turn(late[:, 0:V], a1)
+            shared = bank("both%d" % (j % 2))
+            both = (shared[:, 0:V], shared[:, V : 2 * V])
+            turn(both[0], a0, start=True)
+            turn(both[1], a1)
+            project(part, early)
+            if before:
+                two = join_sums(before[0], one)
+            project(part + 1, late)
+
+            y = bring(n + 1)
+            early = cast(part + 2)
+            late = cast(part + 3)
+            if before:
+                last = acc_bank(n + 1)
+                turn_pair(last[:, 0:V], *before[1])
             y2 = fetch(y, third, "y2_%d" % j)
             y1 = fetch(y, second, "y1_%d" % j)
-            if j + 1 < TILES:
-                y = project(1, j + 1, prepare(1, j + 1))
-            turn(early[:, 0:V], y2, stop=True)
-            turn(late[:, 0:V], y2)
-            turn(late[:, V : 2 * V], y1, stop=True)
-            sum_pairs(j, early, late)
+            turn(both[0], y2)
+            turn(both[1], y2, stop=True)
+            project(part + 2, early)
+            if before:
+                close_sums(j - 1, 0, last[:, 0:V], two[:])
+            project(part + 3, late)
+            before = (both, (a0, y1), shared)
 
-        grouped3 = keep.tile([P, N, PACK], BF16, name="grouped3", align_bytes=64)
-        interleave(grouped3[:], raw3)
-        w3_codes, w3_scales = quantise("w3", grouped3[:].rearrange("p c j -> p (c j)"), N)
+        a1 = fetch(a, second, "a1_%d" % j)
+        two = join_sums(before[0], one)
+        low = bank("both%d" % (j % 2))
+        sums = [
+            (low[:, 0:P], low[:, P : 2 * P], acc_bank(n + 2)[:, 0:P]),
+            (bank("spare0")[:, 0:P], bank("spare1")[:, 0:P], acc_bank(n + 3)[:, 0:P]),
+        ]
+        for h in range(HALVES):
+            cols = slice(h * P, (h + 1) * P)
+            turn_block(sums[h][0], a0[:, cols], start=True)
+            turn_block(sums[h][2], a0[:, cols], start=True)
+        for h in range(HALVES):
+            turn_block(sums[h][1], a1[:, h * P : (h + 1) * P], start=(h == 1))
+        y = bring(n + 1)
+        last = acc_bank(n + 1)
+        turn_pair(last[:, 0:V], *before[1])
+        y2 = keep.tile([P, V], F32, name="y2_%d" % j)
+        for h in range(HALVES):
+            fetch_half(y2[:, h * P : (h + 1) * P], y, third, h)
+        y1 = fetch(y, second, "y1_%d" % j)
+        for h in range(HALVES):
+            turn_block(sums[h][0], y2[:, h * P : (h + 1) * P], stop=(h == 1))
+            turn_block(sums[h][1], y2[:, h * P : (h + 1) * P], stop=True)
+        for h in range(HALVES):
+            turn_block(sums[h][2], y1[:, h * P : (h + 1) * P], stop=True)
+        close_sums(j - 1, 0, last[:, 0:V], two[:])
 
         for h in range(HALVES):
-            pairs = z_turned[h][:].bitcast(F32)
-            back = bank("acc", 4)
+            one = keep.tile([P, P], F32, name="one_last%d" % h)
+            nc.scalar.activation(one[:], sums[h][0], ACT.Relu)
+            two = keep.tile([P, P], F32, name="two_last%d" % h)
+            relu_add(two[:], sums[h][1], one[:])
+            close_sums(TILES - 1, h, sums[h][2], two[:])
+
+        packed = []
+        for h in range(HALVES):
+            back = (acc_bank(2), bank("both0"))[h]
             for u in range(2):
-                nc.tensor.transpose(back[:, u * P : (u + 1) * P], pairs[:, u : H // 2 : 2], ident[:])
+                nc.tensor.transpose(back[:, u * P : (u + 1) * P], z_turned[:, h, u, :].bitcast(F32), ident[:])
             z_grouped = keep.tile([P, P, 2], F32, name="z_grouped%d" % h, align_bytes=64)
-            move = (nc.scalar.copy, nc.vector.tensor_copy)[h]
-            move(z_grouped[:], back[:, 0 : 2 * P].rearrange("p (u v) -> p v u", u=2))
-            z_codes, z_scales = quantise(
-                "z%d" % h, z_grouped[:].rearrange("p v u -> p (v u)").bitcast(BF16), P
-            )
-            acc = bank("acc", 4)
+            nc.scalar.copy(z_grouped[:], back[:, 0 : 2 * P].rearrange("p (u v) -> p v u", u=2))
+            packed.append(z_grouped[:].rearrange("p v u -> p (v u)").bitcast(BF16))
+        for h in range(HALVES):
+            z_codes, z_scales = quantise("z%d" % h, packed[h], P)
+            acc = bank(("both1", "spare0")[h])
             nc.tensor.matmul_mx(
                 out=acc[:, 0:P],
-                lhsT=w3_codes[:].bitcast(FP8X4),
-                lhsT_scale=w3_scales[:],
+                lhsT=weights[PARTS][0],
+                lhsT_scale=weights[PARTS][1],
                 rhs=z_codes[:].bitcast(FP8X4),
                 rhs_scale=z_scales[:],
                 start=True,
                 stop=True,
             )
             result = keep.tile([P, P], F32, name="result%d" % h)
-            if h == 0:
-                nc.scalar.activation(result[:], acc[:, 0:P], ACT.Relu)
-            else:
-                nc.vector.tensor_scalar(result[:], acc[:, 0:P], 0.0, None, ALU.max)
+            nc.scalar.activation(result[:], acc[:, 0:P], ACT.Relu)
             nc.sync.dma_start(out[:, h * P : (h + 1) * P], result[:])

@@ -27,10 +27,23 @@ HALVES = V // P
 BANK = 512
 QUADRANT = 32
 STRIPE = 16
-RUN = 4
+ALIGN = 64
 ACC_BANKS = 4
-HEAD_PARTS = 5
-VECTOR_PARTS = (3,)
+HEAD_PARTS = 2 * PASSES
+LONG_STEPS = (1, 3)
+VECTOR_PARTS = (3, 8)
+GROUPED_TILES = HEAD_PARTS + 1
+
+
+def step_groups(n):
+    start = HEAD_PARTS + PASSES * n + sum(1 for step in LONG_STEPS if step < n)
+    parts = list(range(start, min(start + PASSES + (n in LONG_STEPS), PARTS)))
+    size = 1 if n == 0 else PASSES
+    return [tuple(parts[i : i + size]) for i in range(0, len(parts), size)]
+
+
+def scalar_parts(n):
+    return [i for parts in step_groups(n) for i in parts if i not in VECTOR_PARTS]
 
 
 def tile_picked_yjano_relu_p_kernel(
@@ -39,8 +52,11 @@ def tile_picked_yjano_relu_p_kernel(
     nc = tc.nc
     with ExitStack() as ctx:
         keep = ctx.enter_context(tc.tile_pool(name="keep", bufs=1))
-        ring = ctx.enter_context(tc.tile_pool(name="ring", bufs=2))
+        ring = ctx.enter_context(tc.tile_pool(name="ring", bufs=TILES))
         psum = ctx.enter_context(tc.psum_pool(name="psum", bufs=1))
+
+        def block(i):
+            return slice(i * P, (i + 1) * P)
 
         def load_list(name, source):
             offsets = keep.tile(list(source.shape), U16, name=name)
@@ -48,7 +64,7 @@ def tile_picked_yjano_relu_p_kernel(
             return offsets
 
         def load_words(o):
-            table = keep.tile([P, T], U32, name="words%d" % o, align_bytes=64)
+            table = keep.tile([P, T], U32, name="words%d" % o, align_bytes=ALIGN)
             nc.sync.dma_start(
                 table[:].bitcast(I32),
                 x_words[o].rearrange("p n t -> p (n t)").bitcast(I32),
@@ -58,19 +74,12 @@ def tile_picked_yjano_relu_p_kernel(
         def load_part(i):
             n, o = divmod(i, PASSES)
             j, m = divmod(n, 2)
-            source = (w1, w2)[m][o * K_PASS : (o + 1) * K_PASS, j * P : (j + 1) * P]
-            rows = keep.tile([P, PACK, P], F32, name="raw%d" % i, align_bytes=64)
-            nc.sync.dma_start(rows[:], source.rearrange("(p j) c -> p j c", j=PACK))
+            source = w3 if i == PARTS else (w1, w2)[m][o * K_PASS : (o + 1) * K_PASS, block(j)]
+            rows = keep.tile([P, PACK, P], F32, name="raw%d" % i, align_bytes=ALIGN)
+            nc.sync.dma_start(rows[:], source.rearrange("(p t) c -> p t c", t=PACK))
             return rows
 
-        def load_last():
-            rows = keep.tile([P, PACK, N], F32, name="raw%d" % PARTS, align_bytes=64)
-            dealt = w3.rearrange("(b u r e) c -> u b r (e c)", u=2, r=8, e=2)
-            for u in range(2):
-                nc.sync.dma_start(rows[:, 2 * u : 2 * u + 2, :].rearrange("p e c -> p (e c)"), dealt[u])
-            return rows
-
-        scale_table = keep.tile([P, T], U8, name="scale_table", align_bytes=64)
+        scale_table = keep.tile([P, T], U8, name="scale_table", align_bytes=ALIGN)
         nc.gpsimd.memset(scale_table[:].bitcast(I32), 0)
 
         words0 = load_words(0)
@@ -82,12 +91,11 @@ def tile_picked_yjano_relu_p_kernel(
             )
         raw = [load_part(i) for i in range(PASSES)]
         words1 = load_words(1)
-        raw.extend(load_part(i) for i in range(PASSES, 2 * PASSES))
+        raw.extend(load_part(i) for i in range(PASSES, HEAD_PARTS))
         first = load_list("first", pos1)
         second = load_list("second", pos2)
         third = load_list("third", pos3)
-        raw.extend(load_part(i) for i in range(2 * PASSES, PARTS))
-        raw.append(load_last())
+        raw.extend(load_part(i) for i in range(HEAD_PARTS, PARTS + 1))
 
         ident = keep.tile([P, P], F32, name="ident")
         make_identity(nc, ident[:])
@@ -98,30 +106,43 @@ def tile_picked_yjano_relu_p_kernel(
         def acc_bank(n):
             return bank("acc%d" % (n % ACC_BANKS))
 
-        def cast(i):
-            grouped = ring.tile([P, P, PACK], BF16, name="grouped", bufs=4, align_bytes=64)
-            target = grouped[:].rearrange("p (c i) j -> p c j i", i=RUN)
-            source = raw[i][:].rearrange("p j (c i) -> p c j i", i=RUN)
+        def cast_into(grouped, i):
+            if i == PARTS:
+                target = grouped.rearrange("p (l r) t -> p l t r", r=PACK)
+                source = raw[i][:].rearrange("p t (l r) -> p l t r", r=PACK)
+            else:
+                target = grouped.rearrange("p (u l e) t -> p l t u e", u=2, e=2)
+                source = raw[i][:].rearrange("p t (l u e) -> p l t u e", u=2, e=2)
             if i in VECTOR_PARTS:
                 nc.vector.tensor_copy(target, source)
             else:
-                nc.scalar.activation(target, source, ACT.Copy)
-            return grouped[:].rearrange("p c j -> p (c j)")
+                nc.scalar.copy(target, source)
 
-        def quantise(name, grouped, width):
-            codes = keep.tile([P, width], U32, name=name + "_codes", align_bytes=64)
-            scales = keep.tile([P, width], U8, name=name + "_scales", align_bytes=64)
+        def grouped_tile():
+            return ring.tile([P, PASSES * P, PACK], BF16, name="grouped", bufs=GROUPED_TILES, align_bytes=ALIGN)
+
+        def cast(i):
+            grouped = grouped_tile()
+            cast_into(grouped[:, block(0), :], i)
+            return grouped
+
+        def quantise(name, grouped, width, tag=None):
+            codes = keep.tile([P, width], U32, name=name + "_codes", tag=tag or name + "_codes", align_bytes=ALIGN)
+            scales = keep.tile([P, width], U8, name=name + "_scales", align_bytes=ALIGN)
             nc.vector.quantize_mx(codes[:].bitcast(FP8X4), scales[:], grouped)
             return codes, scales
 
         weights = {}
 
-        def quantise_part(i, grouped):
-            codes, scales = quantise("w%d" % i, grouped, P)
-            weights[i] = (codes[:].bitcast(FP8X4), scales[:])
+        def quantise_parts(parts, grouped, tag=None):
+            width = len(parts) * P
+            flat = grouped[:, 0:width, :].rearrange("p c t -> p (c t)")
+            codes, scales = quantise("w%d" % parts[0], flat, width, tag)
+            for place, i in enumerate(parts):
+                weights[i] = (codes[:, block(place)].bitcast(FP8X4), scales[:, block(place)])
 
-        x_codes = [keep.tile([P, S], U32, name="x_codes0", align_bytes=64)]
-        x_planes = keep.tile([P, S], U8, name="x_planes", align_bytes=64)
+        x_codes = [keep.tile([P, S], U32, name="x_codes0", align_bytes=ALIGN)]
+        x_planes = keep.tile([P, S], U8, name="x_planes", align_bytes=ALIGN)
         accs = {}
 
         def multiply(i, acc, cols):
@@ -136,74 +157,78 @@ def tile_picked_yjano_relu_p_kernel(
                 stop=(o == PASSES - 1),
             )
 
-        def project(i, grouped):
-            quantise_part(i, grouped)
-            if i < PARTS:
+        def project(parts, grouped):
+            quantise_parts(parts, grouped)
+            for i in parts:
                 n = i // PASSES
                 if n not in accs:
                     accs[n] = acc_bank(n)
                 multiply(i, accs[n], slice(0, S))
 
-        def rows_tile():
-            return ring.tile([P, S], F32, name="rows", align_bytes=64)
+        def rows_tile(n):
+            name = "rows%d" % n
+            spent = [PASSES] if n == 0 else scalar_parts(n - 1)[-2:-1]
+            return keep.tile([P, S], F32, name=name, tag="raw%d" % spent[0] if spent else name, align_bytes=ALIGN)
 
         def bring(n):
-            rows = rows_tile()
+            rows = rows_tile(n)
             nc.scalar.copy(rows[:], accs[n][:])
             return rows
 
-        def fetch(rows, offsets, name):
-            got = keep.tile([P, V], F32, name=name)
-            nc.vector.tensor_copy(got[:], rows[:].indirect(offsets[:]))
-            return got
+        def fetched_tag(n):
+            spent = scalar_parts(n - 1)[-1:] if n > 0 else []
+            return "raw%d" % spent[0] if spent and n - 1 != LONG_STEPS[-1] else "fetched%d" % n
 
-        def fetch_half(got, rows, offsets, h):
-            entries = offsets[:, h * P // STRIPE : (h + 1) * P // STRIPE]
-            nc.vector.tensor_copy(got, rows[:].indirect(entries))
+        def fetched_tile(n):
+            return keep.tile([P, 2, V], F32, name="fetched%d" % n, tag=fetched_tag(n), align_bytes=ALIGN)
+
+        def fetch(got, rows, offsets):
+            nc.vector.tensor_copy(got, rows[:].indirect(offsets))
+            return got
 
         def turn_block(target, source, start=False, stop=False):
             nc.tensor.matmul(target, source, ident[:], start=start, stop=stop, is_transpose=True)
 
         def turn(target, source, start=False, stop=False):
             for h in range(HALVES):
-                cols = slice(h * P, (h + 1) * P)
-                turn_block(target[:, cols], source[:, cols], start and h == 0, stop and h == HALVES - 1)
+                turn_block(target[:, block(h)], source[:, block(h)], start and h == 0, stop and h == HALVES - 1)
 
         def turn_pair(target, left, right):
             turn(target, left, start=True)
             turn(target, right, stop=True)
 
-        z_turned = keep.tile([P, HALVES, 2, H // 2], BF16, name="z_turned")
+        z_turned = keep.tile([P, HALVES, 2, H // 2], BF16, name="z_turned", tag="raw%d" % scalar_parts(LONG_STEPS[-1])[-1], align_bytes=ALIGN)
 
         def relu_add(target, sums, other):
             nc.vector.scalar_tensor_tensor(target, sums, 0.0, other, ALU.max, ALU.add)
 
-        def open_sums(both):
+        def relu_of(sums):
             one = ring.tile([P, V], F32, name="one")
-            nc.scalar.activation(one[:], both[0], ACT.Relu)
+            nc.scalar.activation(one[:], sums, ACT.Relu)
             return one
 
-        def join_sums(both, one):
+        def join_sums(sums, one):
             two = ring.tile([P, V], F32, name="two")
-            relu_add(two[:], both[1], one[:])
+            relu_add(two[:], sums, one[:])
             return two
 
-        def by_word(columns, u):
-            return columns.rearrange("p (h g u w) -> p u h g w", g=4, u=2, w=16)[:, u]
-
-        def close_sums(j, first_half, last, two):
-            halves = last.shape[1] // P
-            for u in range(2):
-                target = z_turned[:, first_half : first_half + halves, u, j * P // 2 : (j + 1) * P // 2]
-                relu_add(target.rearrange("p h (g w) -> p h g w", w=16), by_word(last, u), by_word(two, u))
+        def close_sums(j, first_half, sums, two):
+            halves = sums.shape[1] // P
+            target = z_turned[:, first_half : first_half + halves, :, j * P // 2 : (j + 1) * P // 2]
+            relu_add(
+                target.rearrange("p h u w -> p (h u) w"),
+                sums.rearrange("p (r w) -> p r w", w=P // 2),
+                two.rearrange("p (r w) -> p r w", w=P // 2),
+            )
 
         nc.vector.tensor_copy(x_codes[0][:], words0[:].indirect(picked[:]))
         nc.vector.tensor_copy(x_planes[:], scale_table[:].indirect(picked[:]))
-        x_codes.append(keep.tile([P, S], U32, name="x_codes1", align_bytes=64))
+        x_codes.append(keep.tile([P, S], U32, name="x_codes1", align_bytes=ALIGN))
         for i in range(PASSES):
-            quantise_part(i, cast(i))
+            quantise_parts((i,), cast(i))
+
         half_banks = (acc_bank(0), bank("spare0"))
-        a = rows_tile()
+        a = rows_tile(0)
         for h in range(2):
             cols = slice(h * S // 2, (h + 1) * S // 2)
             entries = picked[:, cols.start // STRIPE : cols.stop // STRIPE]
@@ -212,90 +237,103 @@ def tile_picked_yjano_relu_p_kernel(
                 multiply(i, half_banks[h], cols)
             nc.scalar.copy(a[:, cols], half_banks[h][:, cols])
         for i in range(PASSES, HEAD_PARTS):
-            project(i, cast(i))
+            project((i,), cast(i))
+
+        pending = []
+
+        def prepare(n, sums=None):
+            one = None
+            for parts in step_groups(n):
+                if parts[0] not in VECTOR_PARTS:
+                    tag = "grouped%d" % parts[0]
+                grouped = keep.tile([P, PASSES * P, PACK], BF16, name="grouped%d" % parts[0], tag=tag, align_bytes=ALIGN)
+                for place, i in enumerate(parts):
+                    cast_into(grouped[:, block(place), :], i)
+                    if sums is not None and one is None:
+                        one = relu_of(sums)
+                pending.append((parts, grouped))
+            return one
+
+        def project_pending():
+            for group in pending:
+                project(*group)
+            pending.clear()
 
         before = None
         for j in range(TILES):
             n = 2 * j
-            part = HEAD_PARTS + PASSES * n
-            final = j == TILES - 1
             if before:
                 a = bring(n)
-            if not final:
-                early = cast(part)
-            if before:
-                one = open_sums(before[0])
-            if not final:
-                late = cast(part + 1)
-            a0 = fetch(a, first, "a0_%d" % j)
-            if final:
+            project_pending()
+            got = fetched_tile(n)
+            a0 = fetch(got[:, 0, :], a, first[:])
+            if j == TILES - 1:
                 break
-            a1 = fetch(a, second, "a1_%d" % j)
+            a1 = fetch(got[:, 1, :], a, second[:])
+            one = prepare(n, before[0][0] if before else None)
             shared = bank("both%d" % (j % 2))
             both = (shared[:, 0:V], shared[:, V : 2 * V])
             turn(both[0], a0, start=True)
             turn(both[1], a1)
-            project(part, early)
             if before:
-                two = join_sums(before[0], one)
-            project(part + 1, late)
+                two = join_sums(before[0][1], one)
 
             y = bring(n + 1)
-            early = cast(part + 2)
-            late = cast(part + 3)
+            if j == TILES - 2:
+                project_pending()
             if before:
                 last = acc_bank(n + 1)
                 turn_pair(last[:, 0:V], *before[1])
-            y2 = fetch(y, third, "y2_%d" % j)
-            y1 = fetch(y, second, "y1_%d" % j)
+            project_pending()
+            got = fetched_tile(n + 1)
+            y2 = fetch(got[:, 0, :], y, third[:])
+            y1 = fetch(got[:, 1, :], y, second[:])
+            prepare(n + 1)
             turn(both[0], y2)
             turn(both[1], y2, stop=True)
-            project(part + 2, early)
             if before:
                 close_sums(j - 1, 0, last[:, 0:V], two[:])
-            project(part + 3, late)
-            before = (both, (a0, y1), shared)
+            before = (both, (a0, y1))
 
-        a1 = fetch(a, second, "a1_%d" % j)
-        two = join_sums(before[0], one)
-        low = bank("both%d" % (j % 2))
-        sums = [
-            (low[:, 0:P], low[:, P : 2 * P], acc_bank(n + 2)[:, 0:P]),
-            (bank("spare0")[:, 0:P], bank("spare1")[:, 0:P], acc_bank(n + 3)[:, 0:P]),
-        ]
-        for h in range(HALVES):
-            cols = slice(h * P, (h + 1) * P)
-            turn_block(sums[h][0], a0[:, cols], start=True)
-            turn_block(sums[h][2], a0[:, cols], start=True)
-        for h in range(HALVES):
-            turn_block(sums[h][1], a1[:, h * P : (h + 1) * P], start=(h == 1))
+        def after_turns(step, name):
+            return keep.tile([P, V], F32, name=name, tag=fetched_tag(step), align_bytes=ALIGN)
+
         y = bring(n + 1)
+        y2 = fetch(got[:, 1, :], y, third[:])
+        two = join_sums(before[0][1], relu_of(before[0][0]))
         last = acc_bank(n + 1)
         turn_pair(last[:, 0:V], *before[1])
-        y2 = keep.tile([P, V], F32, name="y2_%d" % j)
+        a1 = fetch(after_turns(n - 2, "a1_last")[:], a, second[:])
+        y1 = fetch(after_turns(n - 1, "y1_last")[:], y, second[:])
+        opening = bank("both%d" % (j % 2))[:, 0:V]
+        middle = [bank("spare%d" % h)[:, 0:P] for h in range(HALVES)]
+        closing = [acc_bank(n + 2 + h)[:, 0:P] for h in range(HALVES)]
+        turn(opening, a0, start=True)
         for h in range(HALVES):
-            fetch_half(y2[:, h * P : (h + 1) * P], y, third, h)
-        y1 = fetch(y, second, "y1_%d" % j)
+            turn_block(closing[h], a0[:, block(h)], start=True)
+        turn(opening, y2, stop=True)
         for h in range(HALVES):
-            turn_block(sums[h][0], y2[:, h * P : (h + 1) * P], stop=(h == 1))
-            turn_block(sums[h][1], y2[:, h * P : (h + 1) * P], stop=True)
+            turn_block(middle[h], y2[:, block(h)], start=True)
         for h in range(HALVES):
-            turn_block(sums[h][2], y1[:, h * P : (h + 1) * P], stop=True)
+            turn_block(middle[h], a1[:, block(h)], stop=True)
+        for h in range(HALVES):
+            turn_block(closing[h], y1[:, block(h)], stop=True)
         close_sums(j - 1, 0, last[:, 0:V], two[:])
-
+        one = relu_of(opening)
+        twos = [keep.tile([P, P], F32, name="two_last%d" % h, align_bytes=ALIGN) for h in range(HALVES)]
         for h in range(HALVES):
-            one = keep.tile([P, P], F32, name="one_last%d" % h)
-            nc.scalar.activation(one[:], sums[h][0], ACT.Relu)
-            two = keep.tile([P, P], F32, name="two_last%d" % h)
-            relu_add(two[:], sums[h][1], one[:])
-            close_sums(TILES - 1, h, sums[h][2], two[:])
+            relu_add(twos[h][:], middle[h], one[:, block(h)])
+        for h in range(HALVES):
+            close_sums(j, h, closing[h], twos[h][:])
+
+        quantise_parts((PARTS,), cast(PARTS), tag="two_last%d" % (HALVES - 1))
 
         packed = []
         for h in range(HALVES):
-            back = (acc_bank(2), bank("both0"))[h]
+            back = (acc_bank(n), bank("both0"))[h]
             for u in range(2):
-                nc.tensor.transpose(back[:, u * P : (u + 1) * P], z_turned[:, h, u, :].bitcast(F32), ident[:])
-            z_grouped = keep.tile([P, P, 2], F32, name="z_grouped%d" % h, align_bytes=64)
+                nc.tensor.transpose(back[:, block(u)], z_turned[:, h, u, :].bitcast(F32), ident[:])
+            z_grouped = keep.tile([P, P, 2], F32, name="z_grouped%d" % h, align_bytes=ALIGN)
             nc.scalar.copy(z_grouped[:], back[:, 0 : 2 * P].rearrange("p (u v) -> p v u", u=2))
             packed.append(z_grouped[:].rearrange("p v u -> p (v u)").bitcast(BF16))
         for h in range(HALVES):
@@ -312,4 +350,4 @@ def tile_picked_yjano_relu_p_kernel(
             )
             result = keep.tile([P, P], F32, name="result%d" % h)
             nc.scalar.activation(result[:], acc[:, 0:P], ACT.Relu)
-            nc.sync.dma_start(out[:, h * P : (h + 1) * P], result[:])
+            nc.sync.dma_start(out[:, block(h)], result[:])

@@ -28,22 +28,7 @@ BANK = 512
 QUADRANT = 32
 STRIPE = 16
 ALIGN = 64
-ACC_BANKS = 4
-HEAD_PARTS = 2 * PASSES
-LONG_STEPS = (1, 3)
-VECTOR_PARTS = (3, 8)
-GROUPED_TILES = HEAD_PARTS + 1
-
-
-def step_groups(n):
-    start = HEAD_PARTS + PASSES * n + sum(1 for step in LONG_STEPS if step < n)
-    parts = list(range(start, min(start + PASSES + (n in LONG_STEPS), PARTS)))
-    size = 1 if n == 0 else PASSES
-    return [tuple(parts[i : i + size]) for i in range(0, len(parts), size)]
-
-
-def scalar_parts(n):
-    return [i for parts in step_groups(n) for i in parts if i not in VECTOR_PARTS]
+SCALAR_PARTS = 2
 
 
 def tile_picked_yjano_relu_p_kernel(
@@ -52,11 +37,13 @@ def tile_picked_yjano_relu_p_kernel(
     nc = tc.nc
     with ExitStack() as ctx:
         keep = ctx.enter_context(tc.tile_pool(name="keep", bufs=1))
-        ring = ctx.enter_context(tc.tile_pool(name="ring", bufs=TILES))
         psum = ctx.enter_context(tc.psum_pool(name="psum", bufs=1))
 
         def block(i):
             return slice(i * P, (i + 1) * P)
+
+        def tile(shape, dtype, name, tag=None):
+            return keep.tile(shape, dtype, name=name, tag=tag or name, align_bytes=ALIGN)
 
         def load_list(name, source):
             offsets = keep.tile(list(source.shape), U16, name=name)
@@ -64,7 +51,7 @@ def tile_picked_yjano_relu_p_kernel(
             return offsets
 
         def load_words(o):
-            table = keep.tile([P, T], U32, name="words%d" % o, align_bytes=ALIGN)
+            table = tile([P, T], U32, "words%d" % o)
             nc.sync.dma_start(
                 table[:].bitcast(I32),
                 x_words[o].rearrange("p n t -> p (n t)").bitcast(I32),
@@ -75,27 +62,36 @@ def tile_picked_yjano_relu_p_kernel(
             n, o = divmod(i, PASSES)
             j, m = divmod(n, 2)
             source = w3 if i == PARTS else (w1, w2)[m][o * K_PASS : (o + 1) * K_PASS, block(j)]
-            rows = keep.tile([P, PACK, P], F32, name="raw%d" % i, align_bytes=ALIGN)
+            rows = tile([P, PACK, P], F32, "raw%d" % i)
             nc.sync.dma_start(rows[:], source.rearrange("(p t) c -> p t c", t=PACK))
             return rows
 
-        scale_table = keep.tile([P, T], U8, name="scale_table", align_bytes=ALIGN)
-        nc.gpsimd.memset(scale_table[:].bitcast(I32), 0)
+        scale_table = tile([P, T], U8, "scale_table")
+        nc.gpsimd.memset(scale_table[QUADRANT : 2 * QUADRANT].bitcast(I32), 0)
+        nc.gpsimd.memset(scale_table[2 * QUADRANT :].bitcast(I32), 0)
+        x_planes = tile([P, PASSES, S], U8, "x_planes")
+        nc.vector.memset(x_planes[:].rearrange("p o c -> p (o c)").bitcast(I32), 0)
 
-        words0 = load_words(0)
         picked = load_list("picked", offs)
-        for q in range(P // QUADRANT):
-            nc.sync.dma_start(
-                scale_table[QUADRANT * q : QUADRANT * q + 4 * PASSES, :].bitcast(I32),
-                x_scales[:, 4 * q : 4 * q + 4, :].bitcast(I32),
-            )
+        nc.sync.dma_start(
+            scale_table[0:QUADRANT].bitcast(I32),
+            x_scales.rearrange("o q c -> q o c").bitcast(I32),
+        )
+        words0 = load_words(0)
         raw = [load_part(i) for i in range(PASSES)]
         words1 = load_words(1)
-        raw.extend(load_part(i) for i in range(PASSES, HEAD_PARTS))
         first = load_list("first", pos1)
         second = load_list("second", pos2)
         third = load_list("third", pos3)
-        raw.extend(load_part(i) for i in range(HEAD_PARTS, PARTS + 1))
+        raw.extend(load_part(i) for i in range(PASSES, PARTS + 1))
+
+        x_rows = tile([P, S], U8, "x_rows")
+        nc.vector.tensor_copy(x_rows[:], scale_table[:].indirect(picked[:]))
+        for q in range(P // QUADRANT):
+            nc.scalar.dma_start(
+                x_planes[QUADRANT * q : QUADRANT * q + 4].bitcast(I32),
+                x_rows[4 * PASSES * q : 4 * PASSES * (q + 1)].bitcast(I32),
+            )
 
         ident = keep.tile([P, P], F32, name="ident")
         make_identity(nc, ident[:])
@@ -104,7 +100,8 @@ def tile_picked_yjano_relu_p_kernel(
             return psum.tile([P, BANK], F32, name=tag)
 
         def acc_bank(n):
-            return bank("acc%d" % (n % ACC_BANKS))
+            j, m = divmod(n, 2)
+            return bank("ay"[m] + str(j % 2))
 
         def cast_into(grouped, i):
             if i == PARTS:
@@ -113,37 +110,34 @@ def tile_picked_yjano_relu_p_kernel(
             else:
                 target = grouped.rearrange("p (u l e) t -> p l t u e", u=2, e=2)
                 source = raw[i][:].rearrange("p t (l u e) -> p l t u e", u=2, e=2)
-            if i in VECTOR_PARTS:
-                nc.vector.tensor_copy(target, source)
-            else:
+            if i < SCALAR_PARTS:
                 nc.scalar.copy(target, source)
+            else:
+                nc.vector.tensor_copy(target, source)
 
-        def grouped_tile():
-            return ring.tile([P, PASSES * P, PACK], BF16, name="grouped", bufs=GROUPED_TILES, align_bytes=ALIGN)
+        def grouped_tile(parts):
+            return tile([P, len(parts) * P, PACK], BF16, "grouped%d" % parts[0])
 
-        def cast(i):
-            grouped = grouped_tile()
-            cast_into(grouped[:, block(0), :], i)
+        def cast(parts):
+            grouped = grouped_tile(parts)
+            for place, i in enumerate(parts):
+                cast_into(grouped[:, block(place), :], i)
             return grouped
 
-        def quantise(name, grouped, width, tag=None):
-            codes = keep.tile([P, width], U32, name=name + "_codes", tag=tag or name + "_codes", align_bytes=ALIGN)
-            scales = keep.tile([P, width], U8, name=name + "_scales", align_bytes=ALIGN)
+        def quantise(name, grouped, width):
+            codes = tile([P, width], U32, name + "_codes")
+            scales = tile([P, width], U8, name + "_scales")
             nc.vector.quantize_mx(codes[:].bitcast(FP8X4), scales[:], grouped)
             return codes, scales
 
         weights = {}
 
-        def quantise_parts(parts, grouped, tag=None):
-            width = len(parts) * P
-            flat = grouped[:, 0:width, :].rearrange("p c t -> p (c t)")
-            codes, scales = quantise("w%d" % parts[0], flat, width, tag)
+        def quantise_parts(parts, grouped):
+            codes, scales = quantise("w%d" % parts[0], grouped[:].rearrange("p c t -> p (c t)"), len(parts) * P)
             for place, i in enumerate(parts):
                 weights[i] = (codes[:, block(place)].bitcast(FP8X4), scales[:, block(place)])
 
-        x_codes = [keep.tile([P, S], U32, name="x_codes0", align_bytes=ALIGN)]
-        x_planes = keep.tile([P, S], U8, name="x_planes", align_bytes=ALIGN)
-        accs = {}
+        x_codes = [tile([P, S], U32, "x_codes%d" % o) for o in range(PASSES)]
 
         def multiply(i, acc, cols):
             o = i % PASSES
@@ -152,10 +146,15 @@ def tile_picked_yjano_relu_p_kernel(
                 lhsT=weights[i][0],
                 lhsT_scale=weights[i][1],
                 rhs=x_codes[o][:, cols].bitcast(FP8X4),
-                rhs_scale=x_planes[4 * o :, cols],
+                rhs_scale=x_planes[:, o, cols],
                 start=(o == 0),
                 stop=(o == PASSES - 1),
             )
+
+        accs = {}
+
+        def piece_parts(n):
+            return tuple(range(PASSES * n, PASSES * (n + 1)))
 
         def project(parts, grouped):
             quantise_parts(parts, grouped)
@@ -165,25 +164,20 @@ def tile_picked_yjano_relu_p_kernel(
                     accs[n] = acc_bank(n)
                 multiply(i, accs[n], slice(0, S))
 
-        def rows_tile(n):
-            name = "rows%d" % n
-            spent = [PASSES] if n == 0 else scalar_parts(n - 1)[-2:-1]
-            return keep.tile([P, S], F32, name=name, tag="raw%d" % spent[0] if spent else name, align_bytes=ALIGN)
-
         def bring(n):
-            rows = rows_tile(n)
+            rows = tile([P, S], F32, "rows%d" % n)
             nc.scalar.copy(rows[:], accs[n][:])
             return rows
 
-        def fetched_tag(n):
-            spent = scalar_parts(n - 1)[-1:] if n > 0 else []
-            return "raw%d" % spent[0] if spent and n - 1 != LONG_STEPS[-1] else "fetched%d" % n
+        def codes_of(n):
+            return "w%d_codes" % (PASSES * n)
 
-        def fetched_tile(n):
-            return keep.tile([P, 2, V], F32, name="fetched%d" % n, tag=fetched_tag(n), align_bytes=ALIGN)
-
-        def fetch(got, rows, offsets):
-            nc.vector.tensor_copy(got, rows[:].indirect(offsets))
+        def fetch(name, rows, offsets, on_scalar, tag=None):
+            got = tile([P, V], F32, name, tag)
+            if on_scalar:
+                nc.scalar.activation(got[:], rows[:].indirect(offsets[:]), ACT.Copy)
+            else:
+                nc.vector.tensor_copy(got[:], rows[:].indirect(offsets[:]))
             return got
 
         def turn_block(target, source, start=False, stop=False):
@@ -193,22 +187,18 @@ def tile_picked_yjano_relu_p_kernel(
             for h in range(HALVES):
                 turn_block(target[:, block(h)], source[:, block(h)], start and h == 0, stop and h == HALVES - 1)
 
-        def turn_pair(target, left, right):
-            turn(target, left, start=True)
-            turn(target, right, stop=True)
-
-        z_turned = keep.tile([P, HALVES, 2, H // 2], BF16, name="z_turned", tag="raw%d" % scalar_parts(LONG_STEPS[-1])[-1], align_bytes=ALIGN)
+        z_turned = tile([P, HALVES, 2, H // 2], BF16, "z_turned")
 
         def relu_add(target, sums, other):
             nc.vector.scalar_tensor_tensor(target, sums, 0.0, other, ALU.max, ALU.add)
 
-        def relu_of(sums):
-            one = ring.tile([P, V], F32, name="one")
+        def relu_of(j, sums, tag=None):
+            one = tile([P, V], F32, "one%d" % j, tag)
             nc.scalar.activation(one[:], sums, ACT.Relu)
             return one
 
-        def join_sums(sums, one):
-            two = ring.tile([P, V], F32, name="two")
+        def join_sums(j, sums, one, tag=None):
+            two = tile([P, V], F32, "two%d" % j, tag)
             relu_add(two[:], sums, one[:])
             return two
 
@@ -222,13 +212,11 @@ def tile_picked_yjano_relu_p_kernel(
             )
 
         nc.vector.tensor_copy(x_codes[0][:], words0[:].indirect(picked[:]))
-        nc.vector.tensor_copy(x_planes[:], scale_table[:].indirect(picked[:]))
-        x_codes.append(keep.tile([P, S], U32, name="x_codes1", align_bytes=ALIGN))
         for i in range(PASSES):
-            quantise_parts((i,), cast(i))
+            quantise_parts((i,), cast((i,)))
 
-        half_banks = (acc_bank(0), bank("spare0"))
-        a = rows_tile(0)
+        half_banks = (acc_bank(0), bank("lone1"))
+        a = tile([P, S], F32, "rows0")
         for h in range(2):
             cols = slice(h * S // 2, (h + 1) * S // 2)
             entries = picked[:, cols.start // STRIPE : cols.stop // STRIPE]
@@ -236,109 +224,102 @@ def tile_picked_yjano_relu_p_kernel(
             for i in range(PASSES):
                 multiply(i, half_banks[h], cols)
             nc.scalar.copy(a[:, cols], half_banks[h][:, cols])
-        for i in range(PASSES, HEAD_PARTS):
-            project((i,), cast(i))
+        singles = [cast((i,)) for i in piece_parts(1)]
+        for i, grouped in zip(piece_parts(1), singles):
+            project((i,), grouped)
 
-        pending = []
-
-        def prepare(n, sums=None):
-            one = None
-            for parts in step_groups(n):
-                if parts[0] not in VECTOR_PARTS:
-                    tag = "grouped%d" % parts[0]
-                grouped = keep.tile([P, PASSES * P, PACK], BF16, name="grouped%d" % parts[0], tag=tag, align_bytes=ALIGN)
-                for place, i in enumerate(parts):
-                    cast_into(grouped[:, block(place), :], i)
-                    if sums is not None and one is None:
-                        one = relu_of(sums)
-                pending.append((parts, grouped))
-            return one
-
-        def project_pending():
-            for group in pending:
-                project(*group)
-            pending.clear()
-
-        before = None
-        for j in range(TILES):
-            n = 2 * j
-            if before:
-                a = bring(n)
-            project_pending()
-            got = fetched_tile(n)
-            a0 = fetch(got[:, 0, :], a, first[:])
-            if j == TILES - 1:
-                break
-            a1 = fetch(got[:, 1, :], a, second[:])
-            one = prepare(n, before[0][0] if before else None)
+        def turn_shared(j, a0, a1, y2):
             shared = bank("both%d" % (j % 2))
-            both = (shared[:, 0:V], shared[:, V : 2 * V])
-            turn(both[0], a0, start=True)
-            turn(both[1], a1)
-            if before:
-                two = join_sums(before[0][1], one)
+            turn(shared[:, 0:V], y2, start=True)
+            turn(shared[:, V : 2 * V], y2)
+            turn(shared[:, 0:V], a0)
+            turn(shared[:, V : 2 * V], a1, stop=True)
+            return shared[:, 0:V], shared[:, V : 2 * V]
 
+        def turn_lone(j, a0, y1):
+            lone = bank("lone%d" % (j % 2))[:, 0:V]
+            turn(lone, y1, start=True)
+            turn(lone, a0, stop=True)
+            return lone
+
+        for j in range(TILES - 1):
+            n = 2 * j
+            parts = piece_parts(n + 2)
+            grouped = grouped_tile(parts)
+            if j > 0:
+                a = bring(n)
+                y1 = fetch("y1_%d" % (j - 1), y, second, True, codes_of(n))
+                one = relu_of(j - 1, sums[0], "rows%d" % (n - 1))
+                lone = turn_lone(j - 1, a0, y1)
+            else:
+                a0 = fetch("a0_0", a, first, True)
+                a1 = fetch("a1_0", a, second, True)
+            cast_into(grouped[:, block(0), :], parts[0])
+            if j > 0:
+                a1 = fetch("a1_%d" % j, a, second, False, "raw%d" % (parts[0] - 1))
+            cast_into(grouped[:, block(1), :], parts[1])
+            if j > 0:
+                two = join_sums(j - 1, sums[1], one)
+            project(parts, grouped)
             y = bring(n + 1)
-            if j == TILES - 2:
-                project_pending()
-            if before:
-                last = acc_bank(n + 1)
-                turn_pair(last[:, 0:V], *before[1])
-            project_pending()
-            got = fetched_tile(n + 1)
-            y2 = fetch(got[:, 0, :], y, third[:])
-            y1 = fetch(got[:, 1, :], y, second[:])
-            prepare(n + 1)
-            turn(both[0], y2)
-            turn(both[1], y2, stop=True)
-            if before:
-                close_sums(j - 1, 0, last[:, 0:V], two[:])
-            before = (both, (a0, y1))
+            if j > 0:
+                a0 = fetch("a0_%d" % j, a, first, True, codes_of(n + 1))
+            y2 = fetch("y2_%d" % j, y, third, True)
+            parts = piece_parts(n + 3)
+            groups = [parts] if j < TILES - 2 else [(i,) for i in parts]
+            tiles = [cast(group) for group in groups]
+            for group, grouped in zip(groups[:-1], tiles):
+                project(group, grouped)
+            if j > 0:
+                close_sums(j - 1, 0, lone, two[:])
+            project(groups[-1], tiles[-1])
+            sums = turn_shared(j, a0, a1, y2)
 
-        def after_turns(step, name):
-            return keep.tile([P, V], F32, name=name, tag=fetched_tag(step), align_bytes=ALIGN)
-
+        j = TILES - 1
+        n = 2 * j
+        a = bring(n)
+        y1 = fetch("y1_%d" % (j - 1), y, second, True, codes_of(n))
+        lone = turn_lone(j - 1, a0, y1)
+        grouped = cast((PARTS,))
+        a1 = fetch("a1_%d" % j, a, second, False, "raw%d" % (PARTS - 1))
         y = bring(n + 1)
-        y2 = fetch(got[:, 1, :], y, third[:])
-        two = join_sums(before[0][1], relu_of(before[0][0]))
-        last = acc_bank(n + 1)
-        turn_pair(last[:, 0:V], *before[1])
-        a1 = fetch(after_turns(n - 2, "a1_last")[:], a, second[:])
-        y1 = fetch(after_turns(n - 1, "y1_last")[:], y, second[:])
-        opening = bank("both%d" % (j % 2))[:, 0:V]
-        middle = [bank("spare%d" % h)[:, 0:P] for h in range(HALVES)]
-        closing = [acc_bank(n + 2 + h)[:, 0:P] for h in range(HALVES)]
+        a0 = fetch("a0_%d" % j, a, first, False)
+        one = relu_of(j - 1, sums[0], codes_of(n + 1))
+        y2 = fetch("y2_%d" % j, y, third, True)
+        y1 = fetch("y1_%d" % j, y, second, False)
+        two = join_sums(j - 1, sums[1], one)
+        quantise_parts((PARTS,), grouped)
+        close_sums(j - 1, 0, lone, two[:])
+
+        opening = bank("lone%d" % (j % 2))[:, 0:V]
+        middle = [bank("a%d" % h)[:, 0:P] for h in range(HALVES)]
+        closing = [bank("both1")[:, 0:P], bank("y0")[:, 0:P]]
         turn(opening, a0, start=True)
         for h in range(HALVES):
             turn_block(closing[h], a0[:, block(h)], start=True)
+            turn_block(middle[h], a1[:, block(h)], start=True)
         turn(opening, y2, stop=True)
         for h in range(HALVES):
-            turn_block(middle[h], y2[:, block(h)], start=True)
-        for h in range(HALVES):
-            turn_block(middle[h], a1[:, block(h)], stop=True)
-        for h in range(HALVES):
+            turn_block(middle[h], y2[:, block(h)], stop=True)
             turn_block(closing[h], y1[:, block(h)], stop=True)
-        close_sums(j - 1, 0, last[:, 0:V], two[:])
-        one = relu_of(opening)
-        twos = [keep.tile([P, P], F32, name="two_last%d" % h, align_bytes=ALIGN) for h in range(HALVES)]
+        one = relu_of(j, opening)
+        twos = [tile([P, P], F32, "two_last%d" % h) for h in range(HALVES)]
         for h in range(HALVES):
             relu_add(twos[h][:], middle[h], one[:, block(h)])
         for h in range(HALVES):
             close_sums(j, h, closing[h], twos[h][:])
 
-        quantise_parts((PARTS,), cast(PARTS), tag="two_last%d" % (HALVES - 1))
-
         packed = []
         for h in range(HALVES):
-            back = (acc_bank(n), bank("both0"))[h]
+            back = bank(("y1", "lone0")[h])
             for u in range(2):
                 nc.tensor.transpose(back[:, block(u)], z_turned[:, h, u, :].bitcast(F32), ident[:])
-            z_grouped = keep.tile([P, P, 2], F32, name="z_grouped%d" % h, align_bytes=ALIGN)
+            z_grouped = tile([P, P, 2], F32, "z_grouped%d" % h)
             nc.scalar.copy(z_grouped[:], back[:, 0 : 2 * P].rearrange("p (u v) -> p v u", u=2))
             packed.append(z_grouped[:].rearrange("p v u -> p (v u)").bitcast(BF16))
         for h in range(HALVES):
             z_codes, z_scales = quantise("z%d" % h, packed[h], P)
-            acc = bank(("both1", "spare0")[h])
+            acc = bank(("both0", "lone1")[h])
             nc.tensor.matmul_mx(
                 out=acc[:, 0:P],
                 lhsT=weights[PARTS][0],
@@ -348,6 +329,6 @@ def tile_picked_yjano_relu_p_kernel(
                 start=True,
                 stop=True,
             )
-            result = keep.tile([P, P], F32, name="result%d" % h)
+            result = tile([P, P], F32, "result%d" % h)
             nc.scalar.activation(result[:], acc[:, 0:P], ACT.Relu)
             nc.sync.dma_start(out[:, block(h)], result[:])

@@ -28,7 +28,7 @@ BANK = 512
 QUADRANT = 32
 STRIPE = 16
 ALIGN = 64
-SCALAR_PARTS = 2
+SCALAR_PARTS = 3
 
 
 def tile_picked_yjano_relu_p_kernel(
@@ -78,20 +78,21 @@ def tile_picked_yjano_relu_p_kernel(
             x_scales.rearrange("o q c -> q o c").bitcast(I32),
         )
         words0 = load_words(0)
-        raw = [load_part(i) for i in range(PASSES)]
-        words1 = load_words(1)
-        first = load_list("first", pos1)
-        second = load_list("second", pos2)
-        third = load_list("third", pos3)
-        raw.extend(load_part(i) for i in range(PASSES, PARTS + 1))
+        raw = [load_part(i) for i in range(SCALAR_PARTS)]
 
         x_rows = tile([P, S], U8, "x_rows")
         nc.vector.tensor_copy(x_rows[:], scale_table[:].indirect(picked[:]))
         for q in range(P // QUADRANT):
-            nc.scalar.dma_start(
+            nc.sync.dma_start(
                 x_planes[QUADRANT * q : QUADRANT * q + 4].bitcast(I32),
                 x_rows[4 * PASSES * q : 4 * PASSES * (q + 1)].bitcast(I32),
             )
+
+        words1 = load_words(1)
+        first = load_list("first", pos1)
+        second = load_list("second", pos2)
+        third = load_list("third", pos3)
+        raw.extend(load_part(i) for i in range(SCALAR_PARTS, PARTS + 1))
 
         ident = keep.tile([P, P], F32, name="ident")
         make_identity(nc, ident[:])
@@ -228,20 +229,18 @@ def tile_picked_yjano_relu_p_kernel(
         for i, grouped in zip(piece_parts(1), singles):
             project((i,), grouped)
 
-        def turn_shared(j, a0, a1, y2):
+        def turn_tile(j, a0, a1, y1, y2):
+            opening = acc_bank(2 * j + 2)[:, 0:V]
+            turn(opening, a0, start=True)
+            turn(opening, y2, stop=True)
             shared = bank("both%d" % (j % 2))
-            turn(shared[:, 0:V], y2, start=True)
-            turn(shared[:, V : 2 * V], y2)
-            turn(shared[:, 0:V], a0)
-            turn(shared[:, V : 2 * V], a1, stop=True)
-            return shared[:, 0:V], shared[:, V : 2 * V]
+            turn(shared[:, V : 2 * V], y1, start=True)
+            turn(shared[:, V : 2 * V], a0)
+            turn(shared[:, 0:V], y2)
+            turn(shared[:, 0:V], a1, stop=True)
+            return opening, shared[:, 0:V], shared[:, V : 2 * V]
 
-        def turn_lone(j, a0, y1):
-            lone = bank("lone%d" % (j % 2))[:, 0:V]
-            turn(lone, y1, start=True)
-            turn(lone, a0, stop=True)
-            return lone
-
+        waiting = None
         for j in range(TILES - 1):
             n = 2 * j
             parts = piece_parts(n + 2)
@@ -249,38 +248,37 @@ def tile_picked_yjano_relu_p_kernel(
             if j > 0:
                 a = bring(n)
                 y1 = fetch("y1_%d" % (j - 1), y, second, True, codes_of(n))
-                one = relu_of(j - 1, sums[0], "rows%d" % (n - 1))
-                lone = turn_lone(j - 1, a0, y1)
-            else:
-                a0 = fetch("a0_0", a, first, True)
-                a1 = fetch("a1_0", a, second, True)
+                sums = turn_tile(j - 1, a0, a1, y1, y2)
+            a0 = fetch("a0_%d" % j, a, first, True)
             cast_into(grouped[:, block(0), :], parts[0])
-            if j > 0:
-                a1 = fetch("a1_%d" % j, a, second, False, "raw%d" % (parts[0] - 1))
             cast_into(grouped[:, block(1), :], parts[1])
-            if j > 0:
-                two = join_sums(j - 1, sums[1], one)
+            if waiting:
+                close_sums(*waiting)
             project(parts, grouped)
+            a1 = fetch("a1_%d" % j, a, second, j == 0, "raw%d" % parts[1] if j > 0 else None)
             y = bring(n + 1)
             if j > 0:
-                a0 = fetch("a0_%d" % j, a, first, True, codes_of(n + 1))
+                one = relu_of(j - 1, sums[0], codes_of(n + 1))
             y2 = fetch("y2_%d" % j, y, third, True)
             parts = piece_parts(n + 3)
             groups = [parts] if j < TILES - 2 else [(i,) for i in parts]
             tiles = [cast(group) for group in groups]
             for group, grouped in zip(groups[:-1], tiles):
                 project(group, grouped)
+            if j == TILES - 2:
+                project(groups[-1], tiles[-1])
             if j > 0:
-                close_sums(j - 1, 0, lone, two[:])
-            project(groups[-1], tiles[-1])
-            sums = turn_shared(j, a0, a1, y2)
+                two = join_sums(j - 1, sums[1], one)
+                waiting = (j - 1, 0, sums[2], two[:])
+            if j < TILES - 2:
+                project(groups[-1], tiles[-1])
 
         j = TILES - 1
         n = 2 * j
         a = bring(n)
         y1 = fetch("y1_%d" % (j - 1), y, second, True, codes_of(n))
-        lone = turn_lone(j - 1, a0, y1)
-        grouped = cast((PARTS,))
+        sums = turn_tile(j - 1, a0, a1, y1, y2)
+        close_sums(*waiting)
         a1 = fetch("a1_%d" % j, a, second, False, "raw%d" % (PARTS - 1))
         y = bring(n + 1)
         a0 = fetch("a0_%d" % j, a, first, False)
@@ -288,30 +286,37 @@ def tile_picked_yjano_relu_p_kernel(
         y2 = fetch("y2_%d" % j, y, third, True)
         y1 = fetch("y1_%d" % j, y, second, False)
         two = join_sums(j - 1, sums[1], one)
-        quantise_parts((PARTS,), grouped)
-        close_sums(j - 1, 0, lone, two[:])
+        close_sums(j - 1, 0, sums[2], two[:])
 
-        opening = bank("lone%d" % (j % 2))[:, 0:V]
-        middle = [bank("a%d" % h)[:, 0:P] for h in range(HALVES)]
+        opening = [bank("lone1")[:, 0:P], bank("y1")[:, 0:P]]
+        middle = [bank("a0")[:, 0:P], bank("lone0")[:, 0:P]]
         closing = [bank("both1")[:, 0:P], bank("y0")[:, 0:P]]
-        turn(opening, a0, start=True)
         for h in range(HALVES):
-            turn_block(closing[h], a0[:, block(h)], start=True)
             turn_block(middle[h], a1[:, block(h)], start=True)
-        turn(opening, y2, stop=True)
         for h in range(HALVES):
+            turn_block(opening[h], a0[:, block(h)], start=True)
+            turn_block(closing[h], a0[:, block(h)], start=True)
+        for h in range(HALVES):
+            turn_block(opening[h], y2[:, block(h)], stop=True)
             turn_block(middle[h], y2[:, block(h)], stop=True)
-            turn_block(closing[h], y1[:, block(h)], stop=True)
-        one = relu_of(j, opening)
-        twos = [tile([P, P], F32, "two_last%d" % h) for h in range(HALVES)]
         for h in range(HALVES):
-            relu_add(twos[h][:], middle[h], one[:, block(h)])
+            turn_block(closing[h], y1[:, block(h)], stop=True)
+        twos = []
+        for h in range(HALVES):
+            one = tile([P, P], F32, "one_last%d" % h)
+            nc.scalar.activation(one[:], opening[h], ACT.Relu)
+            twos.append(tile([P, P], F32, "two_last%d" % h))
+            relu_add(twos[h][:], middle[h], one[:])
         for h in range(HALVES):
             close_sums(j, h, closing[h], twos[h][:])
 
+        grouped = tile([P, P, PACK], BF16, "grouped_w3", "two_last0")
+        cast_into(grouped[:], PARTS)
+        quantise_parts((PARTS,), grouped)
+
         packed = []
         for h in range(HALVES):
-            back = bank(("y1", "lone0")[h])
+            back = bank(("a1", "lone1")[h])
             for u in range(2):
                 nc.tensor.transpose(back[:, block(u)], z_turned[:, h, u, :].bitcast(F32), ident[:])
             z_grouped = tile([P, P, 2], F32, "z_grouped%d" % h)
@@ -319,7 +324,7 @@ def tile_picked_yjano_relu_p_kernel(
             packed.append(z_grouped[:].rearrange("p v u -> p (v u)").bitcast(BF16))
         for h in range(HALVES):
             z_codes, z_scales = quantise("z%d" % h, packed[h], P)
-            acc = bank(("both0", "lone1")[h])
+            acc = bank(("both0", "y1")[h])
             nc.tensor.matmul_mx(
                 out=acc[:, 0:P],
                 lhsT=weights[PARTS][0],

@@ -105,15 +105,15 @@ def tile_picked_yjano_relu_p_kernel(
             return bank("ay"[m] + str(j % 2))
 
         def cast_into(grouped, i):
-            if i == PARTS:
-                target = grouped.rearrange("p (l r) t -> p l t r", r=PACK)
-                source = raw[i][:].rearrange("p t (l r) -> p l t r", r=PACK)
-            else:
+            if i < SCALAR_PARTS:
                 target = grouped.rearrange("p (u l e) t -> p l t u e", u=2, e=2)
                 source = raw[i][:].rearrange("p t (l u e) -> p l t u e", u=2, e=2)
-            if i < SCALAR_PARTS:
                 nc.scalar.copy(target, source)
+            elif i == PARTS:
+                nc.vector.tensor_copy(grouped, raw[i][:].rearrange("p t c -> p c t"))
             else:
+                target = grouped.rearrange("p (u l e) t -> p l u e t", u=2, e=2)
+                source = raw[i][:].rearrange("p t (l u e) -> p l u e t", u=2, e=2)
                 nc.vector.tensor_copy(target, source)
 
         def grouped_tile(parts):

@@ -28,7 +28,6 @@ BANK = 512
 QUADRANT = 32
 STRIPE = 16
 ALIGN = 64
-SCALAR_PARTS = 3
 
 
 def tile_picked_yjano_relu_p_kernel(
@@ -78,7 +77,7 @@ def tile_picked_yjano_relu_p_kernel(
             x_scales.rearrange("o q c -> q o c").bitcast(I32),
         )
         words0 = load_words(0)
-        raw = [load_part(i) for i in range(SCALAR_PARTS)]
+        words1 = load_words(1)
 
         x_rows = tile([P, S], U8, "x_rows")
         nc.vector.tensor_copy(x_rows[:], scale_table[:].indirect(picked[:]))
@@ -88,11 +87,11 @@ def tile_picked_yjano_relu_p_kernel(
                 x_rows[4 * PASSES * q : 4 * PASSES * (q + 1)].bitcast(I32),
             )
 
-        words1 = load_words(1)
+        raw = [load_part(i) for i in range(PASSES)]
         first = load_list("first", pos1)
         second = load_list("second", pos2)
         third = load_list("third", pos3)
-        raw.extend(load_part(i) for i in range(SCALAR_PARTS, PARTS + 1))
+        raw.extend(load_part(i) for i in range(PASSES, PARTS + 1))
 
         ident = keep.tile([P, P], F32, name="ident")
         make_identity(nc, ident[:])
@@ -105,11 +104,7 @@ def tile_picked_yjano_relu_p_kernel(
             return bank("ay"[m] + str(j % 2))
 
         def cast_into(grouped, i):
-            if i < SCALAR_PARTS:
-                target = grouped.rearrange("p (u l e) t -> p l t u e", u=2, e=2)
-                source = raw[i][:].rearrange("p t (l u e) -> p l t u e", u=2, e=2)
-                nc.scalar.copy(target, source)
-            elif i == PARTS:
+            if i == PARTS:
                 nc.vector.tensor_copy(grouped, raw[i][:].rearrange("p t c -> p c t"))
             else:
                 target = grouped.rearrange("p (u l e) t -> p l u e t", u=2, e=2)
@@ -212,7 +207,8 @@ def tile_picked_yjano_relu_p_kernel(
                 two.rearrange("p (r w) -> p r w", w=P // 2),
             )
 
-        nc.vector.tensor_copy(x_codes[0][:], words0[:].indirect(picked[:]))
+        for o, words in enumerate((words0, words1)):
+            nc.vector.tensor_copy(x_codes[o][:], words[:].indirect(picked[:]))
         for i in range(PASSES):
             quantise_parts((i,), cast((i,)))
 
@@ -220,8 +216,6 @@ def tile_picked_yjano_relu_p_kernel(
         a = tile([P, S], F32, "rows0")
         for h in range(2):
             cols = slice(h * S // 2, (h + 1) * S // 2)
-            entries = picked[:, cols.start // STRIPE : cols.stop // STRIPE]
-            nc.vector.tensor_copy(x_codes[1][:, cols], words1[:].indirect(entries))
             for i in range(PASSES):
                 multiply(i, half_banks[h], cols)
             nc.scalar.copy(a[:, cols], half_banks[h][:, cols])
@@ -255,7 +249,7 @@ def tile_picked_yjano_relu_p_kernel(
             if waiting:
                 close_sums(*waiting)
             project(parts, grouped)
-            a1 = fetch("a1_%d" % j, a, second, j == 0, "raw%d" % parts[1] if j > 0 else None)
+            a1 = fetch("a1_%d" % j, a, second, j != 1, "raw%d" % parts[1] if j == 1 else None)
             y = bring(n + 1)
             if j > 0:
                 one = relu_of(j - 1, sums[0], codes_of(n + 1))
@@ -279,28 +273,31 @@ def tile_picked_yjano_relu_p_kernel(
         y1 = fetch("y1_%d" % (j - 1), y, second, True, codes_of(n))
         sums = turn_tile(j - 1, a0, a1, y1, y2)
         close_sums(*waiting)
-        a1 = fetch("a1_%d" % j, a, second, False, "raw%d" % (PARTS - 1))
+        a0 = fetch("a0_%d" % j, a, first, False, "raw%d" % (PARTS - 1))
         y = bring(n + 1)
-        a0 = fetch("a0_%d" % j, a, first, False)
+        a1 = fetch("a1_%d" % j, a, second, False)
         one = relu_of(j - 1, sums[0], codes_of(n + 1))
-        y2 = fetch("y2_%d" % j, y, third, True)
-        y1 = fetch("y1_%d" % j, y, second, False)
+        y2 = tile([P, V], F32, "y2_%d" % j)
+        for h in range(HALVES):
+            entries = third[:, h * P // STRIPE : (h + 1) * P // STRIPE]
+            nc.scalar.activation(y2[:, block(h)], y[:].indirect(entries), ACT.Copy)
         two = join_sums(j - 1, sums[1], one)
+        a0_y1 = tile([P, V], F32, "a0_y1", "a1_%d" % (j - 1))
+        nc.vector.tensor_tensor(a0_y1[:], y[:].indirect(second[:]), a0[:], ALU.add)
         close_sums(j - 1, 0, sums[2], two[:])
 
         opening = [bank("lone1")[:, 0:P], bank("y1")[:, 0:P]]
         middle = [bank("a0")[:, 0:P], bank("lone0")[:, 0:P]]
         closing = [bank("both1")[:, 0:P], bank("y0")[:, 0:P]]
         for h in range(HALVES):
-            turn_block(middle[h], a1[:, block(h)], start=True)
-        for h in range(HALVES):
             turn_block(opening[h], a0[:, block(h)], start=True)
-            turn_block(closing[h], a0[:, block(h)], start=True)
+        for h in range(HALVES):
+            turn_block(middle[h], a1[:, block(h)], start=True)
         for h in range(HALVES):
             turn_block(opening[h], y2[:, block(h)], stop=True)
             turn_block(middle[h], y2[:, block(h)], stop=True)
         for h in range(HALVES):
-            turn_block(closing[h], y1[:, block(h)], stop=True)
+            turn_block(closing[h], a0_y1[:, block(h)], start=True, stop=True)
         twos = []
         for h in range(HALVES):
             one = tile([P, P], F32, "one_last%d" % h)

@@ -99,43 +99,38 @@ def tile_picked_yjano_relu_p_kernel(
         def bank(tag):
             return psum.tile([P, BANK], F32, name=tag)
 
-        def acc_bank(n):
-            j, m = divmod(n, 2)
-            return bank("ay"[m] + str(j % 2))
+        grouped = {}
 
-        def cast_into(grouped, i):
+        def cast(i, together=True, tag=None, copy=nc.vector.tensor_copy):
+            key = i - i % PASSES if together else i
+            if key not in grouped:
+                grouped[key] = tile([P, (PASSES if together else 1) * P, PACK], BF16, "grouped%d" % key, tag)
+            target = grouped[key][:, block(i - key), :]
             if i == PARTS:
-                nc.vector.tensor_copy(grouped, raw[i][:].rearrange("p t c -> p c t"))
+                nc.vector.tensor_copy(target, raw[i][:].rearrange("p t c -> p c t"))
             else:
-                target = grouped.rearrange("p (u l e) t -> p l u e t", u=2, e=2)
-                source = raw[i][:].rearrange("p t (l u e) -> p l u e t", u=2, e=2)
-                nc.vector.tensor_copy(target, source)
+                copy(
+                    target.rearrange("p (u l e) t -> p l t u e", u=2, e=2),
+                    raw[i][:].rearrange("p t (l u e) -> p l t u e", u=2, e=2),
+                )
 
-        def grouped_tile(parts):
-            return tile([P, len(parts) * P, PACK], BF16, "grouped%d" % parts[0])
-
-        def cast(parts):
-            grouped = grouped_tile(parts)
-            for place, i in enumerate(parts):
-                cast_into(grouped[:, block(place), :], i)
-            return grouped
-
-        def quantise(name, grouped, width):
-            codes = tile([P, width], U32, name + "_codes")
+        def quantise(name, values, width, tag=None):
+            codes = tile([P, width], U32, name + "_codes", tag)
             scales = tile([P, width], U8, name + "_scales")
-            nc.vector.quantize_mx(codes[:].bitcast(FP8X4), scales[:], grouped)
+            nc.vector.quantize_mx(codes[:].bitcast(FP8X4), scales[:], values)
             return codes, scales
 
         weights = {}
 
-        def quantise_parts(parts, grouped):
-            codes, scales = quantise("w%d" % parts[0], grouped[:].rearrange("p c t -> p (c t)"), len(parts) * P)
-            for place, i in enumerate(parts):
-                weights[i] = (codes[:, block(place)].bitcast(FP8X4), scales[:, block(place)])
+        def quantise_group(key, tag=None):
+            parts = grouped[key].shape[1] // P
+            codes, scales = quantise("w%d" % key, grouped[key][:].rearrange("p c t -> p (c t)"), parts * P, tag)
+            for place in range(parts):
+                weights[key + place] = (codes[:, block(place)].bitcast(FP8X4), scales[:, block(place)])
 
         x_codes = [tile([P, S], U32, "x_codes%d" % o) for o in range(PASSES)]
 
-        def multiply(i, acc, cols):
+        def multiply(i, acc, cols=slice(0, S)):
             o = i % PASSES
             nc.tensor.matmul_mx(
                 out=acc[:, cols],
@@ -149,52 +144,59 @@ def tile_picked_yjano_relu_p_kernel(
 
         accs = {}
 
-        def piece_parts(n):
-            return tuple(range(PASSES * n, PASSES * (n + 1)))
+        def project(n, tag):
+            accs[n] = bank(tag)
+            for o in range(PASSES):
+                multiply(PASSES * n + o, accs[n])
 
-        def project(parts, grouped):
-            quantise_parts(parts, grouped)
-            for i in parts:
-                n = i // PASSES
-                if n not in accs:
-                    accs[n] = acc_bank(n)
-                multiply(i, accs[n], slice(0, S))
+        rows = {}
 
-        def bring(n):
-            rows = tile([P, S], F32, "rows%d" % n)
-            nc.scalar.copy(rows[:], accs[n][:])
-            return rows
+        def bring(n, tag=None):
+            rows[n] = tile([P, S], F32, "rows%d" % n, tag)
+            nc.scalar.copy(rows[n][:], accs[n][:])
 
-        def codes_of(n):
-            return "w%d_codes" % (PASSES * n)
+        got = {}
 
-        def fetch(name, rows, offsets, on_scalar, tag=None):
-            got = tile([P, V], F32, name, tag)
-            if on_scalar:
-                nc.scalar.activation(got[:], rows[:].indirect(offsets[:]), ACT.Copy)
+        def fetch(kind, j, engine, half=None, tag=None, add=None):
+            window = rows[2 * j + (kind[0] == "y")]
+            offsets = dict(a0=first, a1=second, y1=second, y2=third)[kind]
+            name = "%s_%d" % (kind, j) + ("" if half is None else "h%d" % half)
+            width = V if half is None else P
+            target = tile([P, width], F32, name, tag)
+            entries = offsets[:] if half is None else offsets[:, half * P // STRIPE : (half + 1) * P // STRIPE]
+            if engine == "S":
+                nc.scalar.activation(target[:], window[:].indirect(entries), ACT.Copy)
+            elif add:
+                other = got[add, j, half] if half is not None else got[add, j]
+                nc.vector.tensor_tensor(target[:], window[:].indirect(entries), other, ALU.add)
             else:
-                nc.vector.tensor_copy(got[:], rows[:].indirect(offsets[:]))
-            return got
+                nc.vector.tensor_copy(target[:], window[:].indirect(entries))
+            if half is None:
+                got[kind, j] = target[:]
+                for g in range(HALVES):
+                    got[kind, j, g] = target[:, block(g)]
+            else:
+                got[kind, j, half] = target[:]
 
-        def turn_block(target, source, start=False, stop=False):
-            nc.tensor.matmul(target, source, ident[:], start=start, stop=stop, is_transpose=True)
-
-        def turn(target, source, start=False, stop=False):
-            for h in range(HALVES):
-                turn_block(target[:, block(h)], source[:, block(h)], start and h == 0, stop and h == HALVES - 1)
+        def turn(target, kind, j, halves=range(HALVES), start=False, stop=False):
+            for place, g in enumerate(halves):
+                nc.tensor.matmul(
+                    target[:, block(g if target.shape[1] > P else 0)], got[kind, j, g], ident[:],
+                    start=start and place == 0, stop=stop and place == len(halves) - 1, is_transpose=True,
+                )
 
         z_turned = tile([P, HALVES, 2, H // 2], BF16, "z_turned")
 
         def relu_add(target, sums, other):
             nc.vector.scalar_tensor_tensor(target, sums, 0.0, other, ALU.max, ALU.add)
 
-        def relu_of(j, sums, tag=None):
-            one = tile([P, V], F32, "one%d" % j, tag)
+        def relu_of(name, sums, tag=None):
+            one = tile([P, sums.shape[1]], F32, "one" + name, tag)
             nc.scalar.activation(one[:], sums, ACT.Relu)
             return one
 
-        def join_sums(j, sums, one, tag=None):
-            two = tile([P, V], F32, "two%d" % j, tag)
+        def join_sums(name, sums, one, tag=None):
+            two = tile([P, sums.shape[1]], F32, "two" + name, tag)
             relu_add(two[:], sums, one[:])
             return two
 
@@ -204,124 +206,191 @@ def tile_picked_yjano_relu_p_kernel(
             relu_add(
                 target.rearrange("p h u w -> p (h u) w"),
                 sums.rearrange("p (r w) -> p r w", w=P // 2),
-                two.rearrange("p (r w) -> p r w", w=P // 2),
+                two[:].rearrange("p (r w) -> p r w", w=P // 2),
             )
+
+        def pair_sums(j, tag, halves=range(HALVES)):
+            both = bank(tag)
+            w = len(halves) * P
+            turn(both[:, 0:w], "a0", j, halves, start=True)
+            turn(both[:, w : 2 * w], "a1", j, halves)
+            turn(both[:, 0:w], "y2", j, halves)
+            turn(both[:, w : 2 * w], "y2", j, halves, stop=True)
+            return both[:, 0:w], both[:, w : 2 * w]
+
+        def open_sum(tag, kind, j, halves=range(HALVES)):
+            lone = bank(tag)[:, 0 : len(halves) * P]
+            turn(lone, kind, j, halves, start=True)
+            return lone
+
+        def piece(n, tag, early=None, late=None, mid=None):
+            i = PASSES * n
+            accs[n] = bank(tag)
+            cast(i, False)
+            if early:
+                early()
+            cast(i + 1, False)
+            quantise_group(i)
+            multiply(i, accs[n])
+            if late:
+                late()
+            quantise_group(i + 1)
+            multiply(i + 1, accs[n])
+
+        def one_sum(j, tag, halves=range(HALVES)):
+            lone = open_sum(tag, "a0", j, halves)
+            turn(lone, "y2", j, halves, stop=True)
+            return lone
+
+        def two_sums(j, tag, fused):
+            both = bank(tag)
+            turn(both[:, 0:V], "a1", j, start=True)
+            turn(both[:, 0:V], "y2", j)
+            turn(both[:, V : 2 * V], "a0", j, [g for g in range(HALVES) if g not in fused])
+            turn(both[:, V : 2 * V], "y1", j, stop=True)
+            return both[:, 0:V], both[:, V : 2 * V]
+
+        def part(i, acc, filler=None):
+            cast(i, False)
+            if filler:
+                filler()
+            quantise_group(i)
+            multiply(i, acc)
+
+        def first_sum(j, tag):
+            lone = open_sum(tag, "y2", j)
+            turn(lone, "a1", j, stop=True)
+            return lone
+
+        def other_sums(j, tag, fused):
+            both = bank(tag)
+            turn(both[:, 0:V], "a0", j, start=True)
+            turn(both[:, 0:V], "y2", j)
+            turn(both[:, V : 2 * V], "a0", j, [g for g in range(HALVES) if g not in fused])
+            turn(both[:, V : 2 * V], "y1", j, stop=True)
+            return both[:, 0:V], both[:, V : 2 * V]
+
+        def lone_sum(j, tag, fused, halves=range(HALVES)):
+            lone = bank(tag)[:, 0 : len(halves) * P]
+            if not fused:
+                turn(lone, "a0", j, halves, start=True)
+            turn(lone, "y1", j, halves, start=fused, stop=True)
+            return lone
 
         for o, words in enumerate((words0, words1)):
             nc.vector.tensor_copy(x_codes[o][:], words[:].indirect(picked[:]))
+        cast(0, False, copy=nc.scalar.copy)
+        cast(1, False)
         for i in range(PASSES):
-            quantise_parts((i,), cast((i,)))
+            quantise_group(i)
+        half_banks = (bank("b0"), bank("b3"))
+        halves0 = [slice(g * S // 2, (g + 1) * S // 2) for g in range(2)]
+        for i in range(PASSES):
+            for g in range(2):
+                multiply(i, half_banks[g], halves0[g])
+        accs[1] = bank("b1")
+        part(2, accs[1])
+        rows[0] = tile([P, S], F32, "rows0", "grouped2")
+        nc.scalar.copy(rows[0][:, halves0[0]], half_banks[0][:, halves0[0]])
+        part(3, accs[1], lambda: nc.vector.tensor_copy(rows[0][:, halves0[1]], half_banks[1][:, halves0[1]]))
 
-        half_banks = (acc_bank(0), bank("lone1"))
-        a = tile([P, S], F32, "rows0")
-        for h in range(2):
-            cols = slice(h * S // 2, (h + 1) * S // 2)
-            for i in range(PASSES):
-                multiply(i, half_banks[h], cols)
-            nc.scalar.copy(a[:, cols], half_banks[h][:, cols])
-        singles = [cast((i,)) for i in piece_parts(1)]
-        for i, grouped in zip(piece_parts(1), singles):
-            project((i,), grouped)
-
-        def turn_tile(j, a0, a1, y1, y2):
-            opening = acc_bank(2 * j + 2)[:, 0:V]
-            turn(opening, a0, start=True)
-            turn(opening, y2, stop=True)
-            shared = bank("both%d" % (j % 2))
-            turn(shared[:, V : 2 * V], y1, start=True)
-            turn(shared[:, V : 2 * V], a0)
-            turn(shared[:, 0:V], y2)
-            turn(shared[:, 0:V], a1, stop=True)
-            return opening, shared[:, 0:V], shared[:, V : 2 * V]
-
-        waiting = None
-        for j in range(TILES - 1):
-            n = 2 * j
-            parts = piece_parts(n + 2)
-            grouped = grouped_tile(parts)
-            if j > 0:
-                a = bring(n)
-                y1 = fetch("y1_%d" % (j - 1), y, second, True, codes_of(n))
-                sums = turn_tile(j - 1, a0, a1, y1, y2)
-            a0 = fetch("a0_%d" % j, a, first, True)
-            cast_into(grouped[:, block(0), :], parts[0])
-            cast_into(grouped[:, block(1), :], parts[1])
-            if waiting:
-                close_sums(*waiting)
-            project(parts, grouped)
-            a1 = fetch("a1_%d" % j, a, second, j != 1, "raw%d" % parts[1] if j == 1 else None)
-            y = bring(n + 1)
-            if j > 0:
-                one = relu_of(j - 1, sums[0], codes_of(n + 1))
-            y2 = fetch("y2_%d" % j, y, third, True)
-            parts = piece_parts(n + 3)
-            groups = [parts] if j < TILES - 2 else [(i,) for i in parts]
-            tiles = [cast(group) for group in groups]
-            for group, grouped in zip(groups[:-1], tiles):
-                project(group, grouped)
-            if j == TILES - 2:
-                project(groups[-1], tiles[-1])
-            if j > 0:
-                two = join_sums(j - 1, sums[1], one)
-                waiting = (j - 1, 0, sums[2], two[:])
-            if j < TILES - 2:
-                project(groups[-1], tiles[-1])
-
-        j = TILES - 1
-        n = 2 * j
-        a = bring(n)
-        y1 = fetch("y1_%d" % (j - 1), y, second, True, codes_of(n))
-        sums = turn_tile(j - 1, a0, a1, y1, y2)
-        close_sums(*waiting)
-        a0 = fetch("a0_%d" % j, a, first, False, "raw%d" % (PARTS - 1))
-        y = bring(n + 1)
-        a1 = fetch("a1_%d" % j, a, second, False)
-        one = relu_of(j - 1, sums[0], codes_of(n + 1))
-        y2 = tile([P, V], F32, "y2_%d" % j)
-        for h in range(HALVES):
-            entries = third[:, h * P // STRIPE : (h + 1) * P // STRIPE]
-            nc.scalar.activation(y2[:, block(h)], y[:].indirect(entries), ACT.Copy)
-        two = join_sums(j - 1, sums[1], one)
-        a0_y1 = tile([P, V], F32, "a0_y1", "a1_%d" % (j - 1))
-        nc.vector.tensor_tensor(a0_y1[:], y[:].indirect(second[:]), a0[:], ALU.add)
-        close_sums(j - 1, 0, sums[2], two[:])
-
-        opening = [bank("lone1")[:, 0:P], bank("y1")[:, 0:P]]
-        middle = [bank("a0")[:, 0:P], bank("lone0")[:, 0:P]]
-        closing = [bank("both1")[:, 0:P], bank("y0")[:, 0:P]]
-        for h in range(HALVES):
-            turn_block(opening[h], a0[:, block(h)], start=True)
-        for h in range(HALVES):
-            turn_block(middle[h], a1[:, block(h)], start=True)
-        for h in range(HALVES):
-            turn_block(opening[h], y2[:, block(h)], stop=True)
-            turn_block(middle[h], y2[:, block(h)], stop=True)
-        for h in range(HALVES):
-            turn_block(closing[h], a0_y1[:, block(h)], start=True, stop=True)
-        twos = []
-        for h in range(HALVES):
-            one = tile([P, P], F32, "one_last%d" % h)
-            nc.scalar.activation(one[:], opening[h], ACT.Relu)
-            twos.append(tile([P, P], F32, "two_last%d" % h))
-            relu_add(twos[h][:], middle[h], one[:])
-        for h in range(HALVES):
-            close_sums(j, h, closing[h], twos[h][:])
-
-        grouped = tile([P, P, PACK], BF16, "grouped_w3", "two_last0")
-        cast_into(grouped[:], PARTS)
-        quantise_parts((PARTS,), grouped)
+        f = lambda *a, **k: (lambda: fetch(*a, **k))
+        fetch("a0", 0, "S")
+        bring(1)
+        accs[2] = bank("b2")
+        part(4, accs[2], f("a1", 0, "V", 0, "raw3"))
+        part(5, accs[2], f("a1", 0, "V", 1, "raw4"))
+        fetch("y2", 0, "S")
+        o0 = first_sum(0, "b4")
+        bring(2)
+        fetch("y1", 0, "S", 1, tag="w5_codes")
+        fetch("a0", 1, "S")
+        piece(3, "b0", f("y1", 0, "V", 0, "raw5", "a0"))
+        s0 = other_sums(0, "b2", [0])
+        bring(3)
+        one0 = relu_of("0", o0, "w7_codes")
+        fetch("y2", 1, "S")
+        accs[4] = bank("b3")
+        part(8, accs[4], f("a1", 1, "V", 0, "raw7"))
+        part(9, accs[4], f("a1", 1, "V", 1, "raw8"))
+        o1 = first_sum(1, "b4")
+        bring(4)
+        fetch("y1", 1, "S", tag="w9_codes")
+        fetch("a0", 2, "S")
+        accs[5] = bank("b1")
+        cast(10, False)
+        two0 = join_sums("0", s0[0], one0, "raw9")
+        cast(11, False)
+        quantise_group(10)
+        multiply(10, accs[5])
+        quantise_group(11)
+        multiply(11, accs[5])
+        close_sums(0, 0, s0[1], two0)
+        s1 = other_sums(1, "b2", [])
+        bring(5)
+        one1 = relu_of("1", o1, "w11_codes")
+        fetch("y2", 2, "S")
+        accs[6] = bank("b3")
+        part(12, accs[6], f("a1", 2, "V", 0, "raw11"))
+        part(13, accs[6], f("a1", 2, "V", 1, "raw12"))
+        o2 = first_sum(2, "b4")
+        bring(6)
+        fetch("y1", 2, "S", 1, tag="w13_codes")
+        fetch("a0", 3, "S")
+        i = 14
+        cast(i, False)
+        cast(i + 1, False)
+        quantise_group(i)
+        quantise_group(i + 1)
+        fetch("y1", 2, "V", 0, add="a0", tag="raw15")
+        two1 = join_sums("1", s1[0], one1, "raw14")
+        fetch("a1", 3, "V", 1)
+        hb = (bank("b0"), bank("b1"))
+        rows[7] = tile([P, S], F32, "rows7")
+        for g in range(2):
+            multiply(i, hb[g], slice(g * V, (g + 1) * V))
+        for g in range(2):
+            multiply(i + 1, hb[g], slice(g * V, (g + 1) * V))
+        s2 = other_sums(2, "b3", [0])
+        nc.scalar.copy(rows[7][:, 0:V], hb[0][:, 0:V])
+        nc.vector.tensor_copy(rows[7][:, V:S], hb[1][:, V:S])
+        one2 = relu_of("2", o2, "w15_codes")
+        close_sums(1, 0, s1[1], two1)
+        fetch("y2", 3, "S", 0)
+        fetch("y2", 3, "S", 1)
+        fetch("a1", 3, "S", 0, tag="w15_scales")
+        fetch("y1", 3, "V", 0, add="a0")
+        two2 = join_sums("2", s2[0], one2)
+        fetch("y1", 3, "V", 1, add="a0")
+        p = [open_sum(("b5", "b6")[g], "a0", 3, [g]) for g in range(2)]
+        r1 = open_sum("b7", "a1", 3, [1])
+        turn(p[0], "y2", 3, [0], stop=True)
+        l30 = lone_sum(3, "b0", True, [0])
+        turn(p[1], "y2", 3, [1], stop=True)
+        turn(r1, "y2", 3, [1], stop=True)
+        r0 = open_sum("b4", "y2", 3, [0])
+        l31 = lone_sum(3, "b1", True, [1])
+        turn(r0, "a1", 3, [0], stop=True)
+        ones = [relu_of("3h%d" % g, p[g]) for g in range(2)]
+        close_sums(2, 0, s2[1], two2)
+        t0 = join_sums("3h0", l30, ones[0])
+        t1 = join_sums("3h1", r1, ones[1])
+        close_sums(3, 0, r0, t0)
+        close_sums(3, 1, l31, t1)
+        cast(PARTS, False, "two3h0")
+        quantise_group(PARTS)
 
         packed = []
-        for h in range(HALVES):
-            back = bank(("a1", "lone1")[h])
+        for g in range(HALVES):
+            back = bank(("b2", "b3")[g])
             for u in range(2):
-                nc.tensor.transpose(back[:, block(u)], z_turned[:, h, u, :].bitcast(F32), ident[:])
-            z_grouped = tile([P, P, 2], F32, "z_grouped%d" % h)
+                nc.tensor.transpose(back[:, block(u)], z_turned[:, g, u, :].bitcast(F32), ident[:])
+            z_grouped = tile([P, P, 2], F32, "z_grouped%d" % g)
             nc.scalar.copy(z_grouped[:], back[:, 0 : 2 * P].rearrange("p (u v) -> p v u", u=2))
             packed.append(z_grouped[:].rearrange("p v u -> p (v u)").bitcast(BF16))
-        for h in range(HALVES):
-            z_codes, z_scales = quantise("z%d" % h, packed[h], P)
-            acc = bank(("both0", "y1")[h])
+        for g in range(HALVES):
+            z_codes, z_scales = quantise("z%d" % g, packed[g], P)
+            acc = bank(("b5", "b6")[g])
             nc.tensor.matmul_mx(
                 out=acc[:, 0:P],
                 lhsT=weights[PARTS][0],
@@ -331,6 +400,6 @@ def tile_picked_yjano_relu_p_kernel(
                 start=True,
                 stop=True,
             )
-            result = tile([P, P], F32, "result%d" % h)
+            result = tile([P, P], F32, "result%d" % g)
             nc.scalar.activation(result[:], acc[:, 0:P], ACT.Relu)
-            nc.sync.dma_start(out[:, block(h)], result[:])
+            nc.sync.dma_start(out[:, block(g)], result[:])

@@ -20,14 +20,12 @@ P = 128
 PACK = 4
 K_PASS = P * PACK
 PASSES = K // K_PASS
-TILES = H // P
-PIECES = 2 * TILES
-PARTS = PASSES * PIECES
 HALVES = V // P
 BANK = 512
 QUADRANT = 32
 STRIPE = 16
 ALIGN = 64
+TILES = H // P
 
 
 def tile_picked_yjano_relu_p_kernel(
@@ -38,11 +36,14 @@ def tile_picked_yjano_relu_p_kernel(
         keep = ctx.enter_context(tc.tile_pool(name="keep", bufs=1))
         psum = ctx.enter_context(tc.psum_pool(name="psum", bufs=1))
 
-        def block(i):
-            return slice(i * P, (i + 1) * P)
+        def block(i, width=P):
+            return slice(i * width, (i + 1) * width)
 
         def tile(shape, dtype, name, tag=None):
             return keep.tile(shape, dtype, name=name, tag=tag or name, align_bytes=ALIGN)
+
+        def bank(tag):
+            return psum.tile([P, BANK], F32, name=tag)
 
         def load_list(name, source):
             offsets = keep.tile(list(source.shape), U16, name=name)
@@ -51,132 +52,138 @@ def tile_picked_yjano_relu_p_kernel(
 
         def load_words(o):
             table = tile([P, T], U32, "words%d" % o)
-            nc.sync.dma_start(
-                table[:].bitcast(I32),
-                x_words[o].rearrange("p n t -> p (n t)").bitcast(I32),
-            )
+            nc.sync.dma_start(table[:].bitcast(I32), x_words[o].rearrange("p n t -> p (n t)").bitcast(I32))
             return table
 
-        def load_part(i):
-            n, o = divmod(i, PASSES)
-            j, m = divmod(n, 2)
-            source = w3 if i == PARTS else (w1, w2)[m][o * K_PASS : (o + 1) * K_PASS, block(j)]
-            rows = tile([P, PACK, P], F32, "raw%d" % i)
+        raw = {}
+
+        def load(part, count=1):
+            m, j, o = part[0], int(part[1]), int(part[2])
+            source = dict(a=w1, y=w2)[m][block(o, K_PASS), j * P : (j + count) * P]
+            rows = tile([P, PACK, count * P], F32, "raw" + part)
             nc.sync.dma_start(rows[:], source.rearrange("(p t) c -> p t c", t=PACK))
-            return rows
+            for n in range(count):
+                raw["%s%d%d" % (m, j + n, o)] = rows[:, :, block(n)]
+
+        def move_scales(queue):
+            nc.vector.tensor_copy(x_rows[:], scale_table[:].indirect(picked[:]))
+            for q in range(P // QUADRANT):
+                queue.dma_start(
+                    x_planes[QUADRANT * q : QUADRANT * q + 4].bitcast(I32),
+                    x_rows[4 * PASSES * q : 4 * PASSES * (q + 1)].bitcast(I32),
+                )
 
         scale_table = tile([P, T], U8, "scale_table")
         nc.gpsimd.memset(scale_table[QUADRANT : 2 * QUADRANT].bitcast(I32), 0)
         nc.gpsimd.memset(scale_table[2 * QUADRANT :].bitcast(I32), 0)
         x_planes = tile([P, PASSES, S], U8, "x_planes")
         nc.vector.memset(x_planes[:].rearrange("p o c -> p (o c)").bitcast(I32), 0)
+        x_rows = tile([P, S], U8, "x_rows")
 
         picked = load_list("picked", offs)
-        nc.sync.dma_start(
-            scale_table[0:QUADRANT].bitcast(I32),
-            x_scales.rearrange("o q c -> q o c").bitcast(I32),
-        )
-        words0 = load_words(0)
-        words1 = load_words(1)
-
-        x_rows = tile([P, S], U8, "x_rows")
-        nc.vector.tensor_copy(x_rows[:], scale_table[:].indirect(picked[:]))
-        for q in range(P // QUADRANT):
-            nc.sync.dma_start(
-                x_planes[QUADRANT * q : QUADRANT * q + 4].bitcast(I32),
-                x_rows[4 * PASSES * q : 4 * PASSES * (q + 1)].bitcast(I32),
-            )
-
-        raw = [load_part(i) for i in range(PASSES)]
+        nc.sync.dma_start(scale_table[0:QUADRANT].bitcast(I32), x_scales.rearrange("o q c -> q o c").bitcast(I32))
+        words = [load_words(o) for o in range(PASSES)]
+        move_scales(nc.sync)
+        load("a00")
+        load("a01")
         first = load_list("first", pos1)
         second = load_list("second", pos2)
         third = load_list("third", pos3)
-        raw.extend(load_part(i) for i in range(PASSES, PARTS + 1))
+        for part in ("y00", "y01", "a10", "a11", "y10", "y11", "a20", "a21", "y20", "y21", "a30", "a31", "y30", "y31"):
+            load(part)
+        raw3 = tile([P, PACK, N], F32, "raw_w3")
+        nc.sync.dma_start(raw3[:], w3.rearrange("(p t) c -> p t c", t=PACK))
 
         ident = keep.tile([P, P], F32, name="ident")
         make_identity(nc, ident[:])
 
-        def bank(tag):
-            return psum.tile([P, BANK], F32, name=tag)
+        x_codes = [tile([P, S], U32, "x_codes%d" % o) for o in range(PASSES)]
 
-        grouped = {}
+        def pick(o, cols=slice(0, S)):
+            entries = picked[:, cols.start // STRIPE : cols.stop // STRIPE]
+            nc.vector.tensor_copy(x_codes[o][:, cols], words[o][:].indirect(entries))
 
-        def cast(i, together=True, tag=None, copy=nc.vector.tensor_copy):
-            key = i - i % PASSES if together else i
-            if key not in grouped:
-                grouped[key] = tile([P, (PASSES if together else 1) * P, PACK], BF16, "grouped%d" % key, tag)
-            target = grouped[key][:, block(i - key), :]
-            if i == PARTS:
-                nc.vector.tensor_copy(target, raw[i][:].rearrange("p t c -> p c t"))
-            else:
-                copy(
-                    target.rearrange("p (u l e) t -> p l t u e", u=2, e=2),
-                    raw[i][:].rearrange("p t (l u e) -> p l t u e", u=2, e=2),
-                )
+        groups = {}
+        home = {}
+
+        def group(*parts):
+            values = tile([P, len(parts) * P, PACK], BF16, "grouped" + parts[0])
+            groups[parts[0]] = (values, parts)
+            for place, part in enumerate(parts):
+                home[part] = values[:, block(place), :]
+
+        def cast(part, engine="V"):
+            if part not in home:
+                group(part)
+            copy = dict(V=nc.vector.tensor_copy, S=nc.scalar.copy)[engine]
+            copy(
+                home[part].rearrange("p (u l e) t -> p l t u e", u=2, e=2),
+                raw[part].rearrange("p t (l u e) -> p l t u e", u=2, e=2),
+            )
 
         def quantise(name, values, width, tag=None):
-            codes = tile([P, width], U32, name + "_codes", tag)
-            scales = tile([P, width], U8, name + "_scales")
+            codes = tile([P, width], U32, "codes" + name, tag)
+            scales = tile([P, width], U8, "scales" + name)
             nc.vector.quantize_mx(codes[:].bitcast(FP8X4), scales[:], values)
             return codes, scales
 
         weights = {}
 
-        def quantise_group(key, tag=None):
-            parts = grouped[key].shape[1] // P
-            codes, scales = quantise("w%d" % key, grouped[key][:].rearrange("p c t -> p (c t)"), parts * P, tag)
-            for place in range(parts):
-                weights[key + place] = (codes[:, block(place)].bitcast(FP8X4), scales[:, block(place)])
+        def quant(name, tag=None):
+            values, parts = groups[name]
+            codes, scales = quantise(name, values[:].rearrange("p c t -> p (c t)"), len(parts) * P, tag)
+            for place, part in enumerate(parts):
+                weights[part] = (codes[:, block(place)].bitcast(FP8X4), scales[:, block(place)])
 
-        x_codes = [tile([P, S], U32, "x_codes%d" % o) for o in range(PASSES)]
+        accs = {}
+        spans = [slice(0, 256), slice(256, 512), slice(256, 384), slice(384, 512)]
 
-        def multiply(i, acc, cols=slice(0, S)):
-            o = i % PASSES
+        def multiply(part, tag=None, half=None):
+            o = int(part[2])
+            key = part[:2] if half is None else part[:2] + str(half)
+            cols = slice(0, S) if half is None else spans[half]
+            if o == 0:
+                accs[key] = bank(tag)
             nc.tensor.matmul_mx(
-                out=acc[:, cols],
-                lhsT=weights[i][0],
-                lhsT_scale=weights[i][1],
+                out=accs[key][:, cols],
+                lhsT=weights[part][0],
+                lhsT_scale=weights[part][1],
                 rhs=x_codes[o][:, cols].bitcast(FP8X4),
                 rhs_scale=x_planes[:, o, cols],
                 start=(o == 0),
                 stop=(o == PASSES - 1),
             )
 
-        accs = {}
-
-        def project(n, tag):
-            accs[n] = bank(tag)
-            for o in range(PASSES):
-                multiply(PASSES * n + o, accs[n])
-
         rows = {}
 
-        def bring(n, tag=None):
-            rows[n] = tile([P, S], F32, "rows%d" % n, tag)
-            nc.scalar.copy(rows[n][:], accs[n][:])
+        def bring(piece, engine="S", tag=None, half=None):
+            if piece not in rows:
+                rows[piece] = tile([P, S], F32, "rows" + piece, tag)
+            copy = dict(V=nc.vector.tensor_copy, S=nc.scalar.copy)[engine]
+            if half is None:
+                copy(rows[piece][:], accs[piece][:])
+            else:
+                cols = spans[half]
+                copy(rows[piece][:, cols], accs[piece + str(half)][:, cols])
 
         got = {}
 
-        def fetch(kind, j, engine, half=None, tag=None, add=None):
-            window = rows[2 * j + (kind[0] == "y")]
+        def fetch(kind, j, engine, half=None, tag=None, add=None, into=None):
+            window = rows[kind[0] + str(j)]
             offsets = dict(a0=first, a1=second, y1=second, y2=third)[kind]
             name = "%s_%d" % (kind, j) + ("" if half is None else "h%d" % half)
-            width = V if half is None else P
-            target = tile([P, width], F32, name, tag)
-            entries = offsets[:] if half is None else offsets[:, half * P // STRIPE : (half + 1) * P // STRIPE]
+            target = into if into is not None else tile([P, V if half is None else P], F32, name, tag)
+            entries = offsets[:] if half is None else offsets[:, block(half, P // STRIPE)]
             if engine == "S":
                 nc.scalar.activation(target[:], window[:].indirect(entries), ACT.Copy)
             elif add:
-                other = got[add, j, half] if half is not None else got[add, j]
-                nc.vector.tensor_tensor(target[:], window[:].indirect(entries), other, ALU.add)
+                nc.vector.tensor_tensor(target[:], window[:].indirect(entries), got[add, j, half], ALU.add)
             else:
                 nc.vector.tensor_copy(target[:], window[:].indirect(entries))
+            got[kind, j, half] = target[:]
             if half is None:
-                got[kind, j] = target[:]
                 for g in range(HALVES):
                     got[kind, j, g] = target[:, block(g)]
-            else:
-                got[kind, j, half] = target[:]
 
         def turn(target, kind, j, halves=range(HALVES), start=False, stop=False):
             for place, g in enumerate(halves):
@@ -187,9 +194,6 @@ def tile_picked_yjano_relu_p_kernel(
 
         z_turned = tile([P, HALVES, 2, H // 2], BF16, "z_turned")
 
-        def relu_add(target, sums, other):
-            nc.vector.scalar_tensor_tensor(target, sums, 0.0, other, ALU.max, ALU.add)
-
         def relu_of(name, sums, tag=None):
             one = tile([P, sums.shape[1]], F32, "one" + name, tag)
             nc.scalar.activation(one[:], sums, ACT.Relu)
@@ -197,204 +201,41 @@ def tile_picked_yjano_relu_p_kernel(
 
         def join_sums(name, sums, one, tag=None):
             two = tile([P, sums.shape[1]], F32, "two" + name, tag)
-            relu_add(two[:], sums, one[:])
+            nc.vector.scalar_tensor_tensor(two[:], sums, 0.0, one[:], ALU.max, ALU.add)
             return two
 
         def close_sums(j, first_half, sums, two):
             halves = sums.shape[1] // P
-            target = z_turned[:, first_half : first_half + halves, :, j * P // 2 : (j + 1) * P // 2]
-            relu_add(
+            target = z_turned[:, first_half : first_half + halves, :, block(j, P // 2)]
+            nc.vector.scalar_tensor_tensor(
                 target.rearrange("p h u w -> p (h u) w"),
                 sums.rearrange("p (r w) -> p r w", w=P // 2),
+                0.0,
                 two[:].rearrange("p (r w) -> p r w", w=P // 2),
+                ALU.max,
+                ALU.add,
             )
 
-        def pair_sums(j, tag, halves=range(HALVES)):
-            both = bank(tag)
-            w = len(halves) * P
-            turn(both[:, 0:w], "a0", j, halves, start=True)
-            turn(both[:, w : 2 * w], "a1", j, halves)
-            turn(both[:, 0:w], "y2", j, halves)
-            turn(both[:, w : 2 * w], "y2", j, halves, stop=True)
-            return both[:, 0:w], both[:, w : 2 * w]
+        def last_weights(tag=None, copy=nc.vector.tensor_copy):
+            values = tile([P, N, PACK], BF16, "w3_grouped", tag)
+            copy(values[:], raw3[:].rearrange("p t c -> p c t"))
+            return values
 
-        def open_sum(tag, kind, j, halves=range(HALVES)):
-            lone = bank(tag)[:, 0 : len(halves) * P]
-            turn(lone, kind, j, halves, start=True)
-            return lone
-
-        def piece(n, tag, early=None, late=None, mid=None):
-            i = PASSES * n
-            accs[n] = bank(tag)
-            cast(i, False)
-            if early:
-                early()
-            cast(i + 1, False)
-            quantise_group(i)
-            multiply(i, accs[n])
-            if late:
-                late()
-            quantise_group(i + 1)
-            multiply(i + 1, accs[n])
-
-        def one_sum(j, tag, halves=range(HALVES)):
-            lone = open_sum(tag, "a0", j, halves)
-            turn(lone, "y2", j, halves, stop=True)
-            return lone
-
-        def two_sums(j, tag, fused):
-            both = bank(tag)
-            turn(both[:, 0:V], "a1", j, start=True)
-            turn(both[:, 0:V], "y2", j)
-            turn(both[:, V : 2 * V], "a0", j, [g for g in range(HALVES) if g not in fused])
-            turn(both[:, V : 2 * V], "y1", j, stop=True)
-            return both[:, 0:V], both[:, V : 2 * V]
-
-        def part(i, acc, filler=None):
-            cast(i, False)
-            if filler:
-                filler()
-            quantise_group(i)
-            multiply(i, acc)
-
-        def first_sum(j, tag):
-            lone = open_sum(tag, "y2", j)
-            turn(lone, "a1", j, stop=True)
-            return lone
-
-        def other_sums(j, tag, fused):
-            both = bank(tag)
-            turn(both[:, 0:V], "a0", j, start=True)
-            turn(both[:, 0:V], "y2", j)
-            turn(both[:, V : 2 * V], "a0", j, [g for g in range(HALVES) if g not in fused])
-            turn(both[:, V : 2 * V], "y1", j, stop=True)
-            return both[:, 0:V], both[:, V : 2 * V]
-
-        def lone_sum(j, tag, fused, halves=range(HALVES)):
-            lone = bank(tag)[:, 0 : len(halves) * P]
-            if not fused:
-                turn(lone, "a0", j, halves, start=True)
-            turn(lone, "y1", j, halves, start=fused, stop=True)
-            return lone
-
-        for o, words in enumerate((words0, words1)):
-            nc.vector.tensor_copy(x_codes[o][:], words[:].indirect(picked[:]))
-        cast(0, False, copy=nc.scalar.copy)
-        cast(1, False)
-        for i in range(PASSES):
-            quantise_group(i)
-        half_banks = (bank("b0"), bank("b3"))
-        halves0 = [slice(g * S // 2, (g + 1) * S // 2) for g in range(2)]
-        for i in range(PASSES):
-            for g in range(2):
-                multiply(i, half_banks[g], halves0[g])
-        accs[1] = bank("b1")
-        part(2, accs[1])
-        rows[0] = tile([P, S], F32, "rows0", "grouped2")
-        nc.scalar.copy(rows[0][:, halves0[0]], half_banks[0][:, halves0[0]])
-        part(3, accs[1], lambda: nc.vector.tensor_copy(rows[0][:, halves0[1]], half_banks[1][:, halves0[1]]))
-
-        f = lambda *a, **k: (lambda: fetch(*a, **k))
-        fetch("a0", 0, "S")
-        bring(1)
-        accs[2] = bank("b2")
-        part(4, accs[2], f("a1", 0, "V", 0, "raw3"))
-        part(5, accs[2], f("a1", 0, "V", 1, "raw4"))
-        fetch("y2", 0, "S")
-        o0 = first_sum(0, "b4")
-        bring(2)
-        fetch("y1", 0, "S", 1, tag="w5_codes")
-        fetch("a0", 1, "S")
-        piece(3, "b0", f("y1", 0, "V", 0, "raw5", "a0"))
-        s0 = other_sums(0, "b2", [0])
-        bring(3)
-        one0 = relu_of("0", o0, "w7_codes")
-        fetch("y2", 1, "S")
-        accs[4] = bank("b3")
-        part(8, accs[4], f("a1", 1, "V", 0, "raw7"))
-        part(9, accs[4], f("a1", 1, "V", 1, "raw8"))
-        o1 = first_sum(1, "b4")
-        bring(4)
-        fetch("y1", 1, "S", tag="w9_codes")
-        fetch("a0", 2, "S")
-        accs[5] = bank("b1")
-        cast(10, False)
-        two0 = join_sums("0", s0[0], one0, "raw9")
-        cast(11, False)
-        quantise_group(10)
-        multiply(10, accs[5])
-        quantise_group(11)
-        multiply(11, accs[5])
-        close_sums(0, 0, s0[1], two0)
-        s1 = other_sums(1, "b2", [])
-        bring(5)
-        one1 = relu_of("1", o1, "w11_codes")
-        fetch("y2", 2, "S")
-        accs[6] = bank("b3")
-        part(12, accs[6], f("a1", 2, "V", 0, "raw11"))
-        part(13, accs[6], f("a1", 2, "V", 1, "raw12"))
-        o2 = first_sum(2, "b4")
-        bring(6)
-        fetch("y1", 2, "S", 1, tag="w13_codes")
-        fetch("a0", 3, "S")
-        i = 14
-        cast(i, False)
-        cast(i + 1, False)
-        quantise_group(i)
-        quantise_group(i + 1)
-        fetch("y1", 2, "V", 0, add="a0", tag="raw15")
-        two1 = join_sums("1", s1[0], one1, "raw14")
-        fetch("a1", 3, "V", 1)
-        hb = (bank("b0"), bank("b1"))
-        rows[7] = tile([P, S], F32, "rows7")
-        for g in range(2):
-            multiply(i, hb[g], slice(g * V, (g + 1) * V))
-        for g in range(2):
-            multiply(i + 1, hb[g], slice(g * V, (g + 1) * V))
-        s2 = other_sums(2, "b3", [0])
-        nc.scalar.copy(rows[7][:, 0:V], hb[0][:, 0:V])
-        nc.vector.tensor_copy(rows[7][:, V:S], hb[1][:, V:S])
-        one2 = relu_of("2", o2, "w15_codes")
-        close_sums(1, 0, s1[1], two1)
-        fetch("y2", 3, "S", 0)
-        fetch("y2", 3, "S", 1)
-        fetch("a1", 3, "S", 0, tag="w15_scales")
-        fetch("y1", 3, "V", 0, add="a0")
-        two2 = join_sums("2", s2[0], one2)
-        fetch("y1", 3, "V", 1, add="a0")
-        p = [open_sum(("b5", "b6")[g], "a0", 3, [g]) for g in range(2)]
-        r1 = open_sum("b7", "a1", 3, [1])
-        turn(p[0], "y2", 3, [0], stop=True)
-        l30 = lone_sum(3, "b0", True, [0])
-        turn(p[1], "y2", 3, [1], stop=True)
-        turn(r1, "y2", 3, [1], stop=True)
-        r0 = open_sum("b4", "y2", 3, [0])
-        l31 = lone_sum(3, "b1", True, [1])
-        turn(r0, "a1", 3, [0], stop=True)
-        ones = [relu_of("3h%d" % g, p[g]) for g in range(2)]
-        close_sums(2, 0, s2[1], two2)
-        t0 = join_sums("3h0", l30, ones[0])
-        t1 = join_sums("3h1", r1, ones[1])
-        close_sums(3, 0, r0, t0)
-        close_sums(3, 1, l31, t1)
-        cast(PARTS, False, "two3h0")
-        quantise_group(PARTS)
-
-        packed = []
-        for g in range(HALVES):
-            back = bank(("b2", "b3")[g])
+        def turn_back(g, tag):
+            back = bank(tag)
             for u in range(2):
                 nc.tensor.transpose(back[:, block(u)], z_turned[:, g, u, :].bitcast(F32), ident[:])
             z_grouped = tile([P, P, 2], F32, "z_grouped%d" % g)
             nc.scalar.copy(z_grouped[:], back[:, 0 : 2 * P].rearrange("p (u v) -> p v u", u=2))
-            packed.append(z_grouped[:].rearrange("p v u -> p (v u)").bitcast(BF16))
-        for g in range(HALVES):
-            z_codes, z_scales = quantise("z%d" % g, packed[g], P)
-            acc = bank(("b5", "b6")[g])
+            return z_grouped[:].rearrange("p v u -> p (v u)").bitcast(BF16)
+
+        def finish(g, packed, tag):
+            z_codes, z_scales = quantise("z%d" % g, packed, P)
+            acc = bank(tag)
             nc.tensor.matmul_mx(
                 out=acc[:, 0:P],
-                lhsT=weights[PARTS][0],
-                lhsT_scale=weights[PARTS][1],
+                lhsT=w3_codes[:].bitcast(FP8X4),
+                lhsT_scale=w3_scales[:],
                 rhs=z_codes[:].bitcast(FP8X4),
                 rhs_scale=z_scales[:],
                 start=True,
@@ -403,3 +244,123 @@ def tile_picked_yjano_relu_p_kernel(
             result = tile([P, P], F32, "result%d" % g)
             nc.scalar.activation(result[:], acc[:, 0:P], ACT.Relu)
             nc.sync.dma_start(out[:, block(g)], result[:])
+
+        def part(name, tag=None, filler=None):
+            cast(name)
+            if filler:
+                filler()
+            quant(name)
+            multiply(name, tag)
+        def f(*a, **k):
+            return lambda: fetch(*a, **k)
+        def lone(tag, kinds, j, halves=range(HALVES)):
+            o = bank(tag)[:, 0 : len(halves) * P]
+            for n, kind in enumerate(kinds):
+                turn(o, kind, j, halves, start=n == 0, stop=n == len(kinds) - 1)
+            return o
+        def other_sums(j, tag, fused):
+            both = bank(tag)
+            turn(both[:, 0:V], "a0", j, start=True)
+            turn(both[:, 0:V], "y2", j)
+            turn(both[:, V:], "a0", j, [g for g in range(HALVES) if g not in fused])
+            turn(both[:, V:], "y1", j, stop=True)
+            return both[:, 0:V], both[:, V:]
+        pick(0)
+        pick(1)
+        cast("a00", "S")
+        cast("a01")
+        quant("a00")
+        quant("a01")
+        for name in ("a00", "a01"):
+            for g in range(2):
+                multiply(name, ("b0", "b3")[g], g)
+        part("y00", "b1")
+        bring("a0", "S", "groupedy00", half=0)
+        cast("y01")
+        bring("a0", "V", half=1)
+        quant("y01")
+        multiply("y01")
+        fetch("a0", 0, "S")
+        bring("y0")
+        part("a10", "b2", f("a1", 0, "V", 0, "rawy01"))
+        part("a11", None, f("a1", 0, "V", 1, "rawa10"))
+        fetch("y2", 0, "S")
+        o0 = lone("b4", ["y2", "a1"], 0)
+        bring("a1")
+        fetch("y1", 0, "S", 1, tag="codesa11")
+        fetch("a0", 1, "S")
+        part("y10", "b0", f("y1", 0, "V", 0, "rawa11", "a0"))
+        part("y11")
+        s0 = other_sums(0, "b2", [0])
+        bring("y1")
+        one0 = relu_of("0", o0, "codesy11")
+        fetch("y2", 1, "S")
+        part("a20", "b3", f("a1", 1, "V", 0, "rawy11"))
+        part("a21", None, f("a1", 1, "V", 1, "rawa20"))
+        o1 = lone("b4", ["y2", "a1"], 1)
+        bring("a2")
+        fetch("y1", 1, "S", tag="codesa21")
+        fetch("a0", 2, "S")
+        cast("y20")
+        two0 = join_sums("0", s0[0], one0, "rawa21")
+        cast("y21")
+        quant("y20")
+        multiply("y20", "b1")
+        quant("y21")
+        multiply("y21")
+        close_sums(0, 0, s0[1], two0)
+        s1 = other_sums(1, "b2", [])
+        bring("y2")
+        one1 = relu_of("1", o1, "codesy21")
+        fetch("y2", 2, "S")
+        part("a30", "b3", f("a1", 2, "V", 0, "rawy21"))
+        part("a31", None, f("a1", 2, "V", 1, "rawa30"))
+        o2 = lone("b4", ["y2", "a1"], 2)
+        bring("a3")
+        fetch("y1", 2, "S", 1, tag="codesa31")
+        fetch("a0", 3, "S")
+        cast("y30")
+        cast("y31")
+        quant("y30")
+        quant("y31")
+        fetch("y1", 2, "V", 0, add="a0", tag="rawy31")
+        two1 = join_sums("1", s1[0], one1, "rawy30")
+        fetch("a1", 3, "V", 1)
+        for name in ("y30", "y31"):
+            for g in range(2):
+                multiply(name, ("b0", "b1")[g], g)
+        s2 = other_sums(2, "b3", [0])
+        bring("y3", "S", half=0)
+        bring("y3", "V", half=1)
+        one2 = relu_of("2", o2, "codesy31")
+        close_sums(1, 0, s1[1], two1)
+        fetch("a1", 3, "V", 0, tag="scalesy31")
+        fetch("y2", 3, "S", 0)
+        fetch("y2", 3, "V", 1)
+        fetch("y1", 3, "S", 1)
+        two2 = join_sums("2", s2[0], one2)
+        fetch("y1", 3, "V", 0, add="a0")
+        p = [bank(("b5", "b6")[g])[:, 0:P] for g in range(2)]
+        r = [bank(("b4", "b7")[g])[:, 0:P] for g in range(2)]
+        l31 = bank("b2")[:, 0:P]
+        for g in range(2):
+            turn(p[g], "a0", 3, [g], start=True)
+        turn(r[1], "a1", 3, [1], start=True)
+        turn(l31, "a0", 3, [1], start=True)
+        turn(r[0], "a1", 3, [0], start=True)
+        for g in range(2):
+            turn(p[g], "y2", 3, [g], stop=True)
+        for g in range(2):
+            turn(r[g], "y2", 3, [g], stop=True)
+        l30 = lone("b0", ["y1"], 3, [0])
+        turn(l31, "y1", 3, [1], stop=True)
+        ones = [relu_of("3h%d" % g, p[g]) for g in range(2)]
+        close_sums(2, 0, s2[1], two2)
+        twos = [join_sums("3h%d" % g, r[g], ones[g]) for g in range(2)]
+        close_sums(3, 0, l30, twos[0])
+        close_sums(3, 1, l31, twos[1])
+        w3_values = last_weights("two3h0")
+        w3_codes, w3_scales = quantise("w3", w3_values[:].rearrange("p c t -> p (c t)"), N)
+        packed = [turn_back(g, ("b1", "b3")[g]) for g in range(2)]
+        for g in range(2):
+            finish(g, packed[g], ("b5", "b6")[g])

@@ -106,8 +106,8 @@ def tile_picked_yjano_relu_p_kernel(
         groups = {}
         home = {}
 
-        def group(*parts):
-            values = tile([P, len(parts) * P, PACK], BF16, "grouped" + parts[0])
+        def group(*parts, tag=None):
+            values = tile([P, len(parts) * P, PACK], BF16, "grouped" + parts[0], tag)
             groups[parts[0]] = (values, parts)
             for place, part in enumerate(parts):
                 home[part] = values[:, block(place), :]
@@ -270,12 +270,12 @@ def tile_picked_yjano_relu_p_kernel(
         cast("a00", "S")
         cast("a01")
         quant("a00")
-        quant("a01")
+        quant("a01", "groupeda00")
         for name in ("a00", "a01"):
             for g in range(2):
                 multiply(name, ("b0", "b3")[g], g)
         part("y00", "b1")
-        bring("a0", "S", "groupedy00", half=0)
+        bring("a0", "S", "rawy00", half=0)
         cast("y01")
         bring("a0", "V", half=1)
         quant("y01")

@@ -112,13 +112,13 @@ def tile_picked_yjano_relu_p_kernel(
             for place, part in enumerate(parts):
                 home[part] = values[:, block(place), :]
 
-        def cast(part, engine="V"):
+        def cast(part, engine="V", share=slice(None)):
             if part not in home:
                 group(part)
             copy = dict(V=nc.vector.tensor_copy, S=nc.scalar.copy)[engine]
             copy(
-                home[part].rearrange("p (u l e) t -> p l t u e", u=2, e=2),
-                raw[part].rearrange("p t (l u e) -> p l t u e", u=2, e=2),
+                home[part].rearrange("p (u l e) t -> p l t u e", u=2, e=2)[:, share],
+                raw[part].rearrange("p t (l u e) -> p l t u e", u=2, e=2)[:, share],
             )
 
         def quantise(name, values, width, tag=None):
@@ -267,10 +267,11 @@ def tile_picked_yjano_relu_p_kernel(
             return both[:, 0:V], both[:, V:]
         pick(0)
         pick(1)
-        cast("a00", "S")
-        cast("a01")
+        cast("a00")
+        cast("a01", "V", slice(0, 16))
+        cast("a01", "S", slice(16, 32))
         quant("a00")
-        quant("a01", "groupeda00")
+        quant("a01")
         for name in ("a00", "a01"):
             for g in range(2):
                 multiply(name, ("b0", "b3")[g], g)

from contextlib import ExitStack

import concourse.mybir as mybir
from concourse.masks import make_identity

K, T, S, V, H, N = 1024, 2048, 512, 256, 512, 128
FLOPS = 2 * (2 * K * H * S + H * N * V)

F32 = mybir.dt.float32
BF16 = mybir.dt.bfloat16
I32 = mybir.dt.int32
U32 = mybir.dt.uint32
U16 = mybir.dt.uint16
U8 = mybir.dt.uint8
FP8X4 = mybir.dt.float8_e4m3fn_x4
ALU = mybir.AluOpType
ACT = mybir.ActivationFunctionType

P = 128
PACK = 4
K_PASS = P * PACK
PASSES = K // K_PASS
HALVES = V // P
BANK = 512
QUADRANT = 32
STRIPE = 16
ALIGN = 64
TILES = H // P


def tile_picked_yjano_relu_p_kernel(
    tc, x_words, x_scales, w1, w2, w3, offs, pos1, pos2, pos3, out
):
    nc = tc.nc
    with ExitStack() as ctx:
        keep = ctx.enter_context(tc.tile_pool(name="keep", bufs=1))
        psum = ctx.enter_context(tc.psum_pool(name="psum", bufs=1))

        def block(i, width=P):
            return slice(i * width, (i + 1) * width)

        def tile(shape, dtype, name, tag=None):
            return keep.tile(shape, dtype, name=name, tag=tag or name, align_bytes=ALIGN)

        def bank(tag):
            return psum.tile([P, BANK], F32, name=tag)

        def load_list(name, source):
            offsets = keep.tile(list(source.shape), U16, name=name)
            nc.sync.dma_start(offsets[:], source)
            return offsets

        def load_words(o):
            table = tile([P, T], U32, "words%d" % o)
            nc.sync.dma_start(table[:].bitcast(I32), x_words[o].rearrange("p n t -> p (n t)").bitcast(I32))
            return table

        raw = {}

        def load(part, count=1):
            m, j, o = part[0], int(part[1]), int(part[2])
            source = dict(a=w1, y=w2)[m][block(o, K_PASS), j * P : (j + count) * P]
            rows = tile([P, PACK, count * P], F32, "raw" + part)
            nc.sync.dma_start(rows[:], source.rearrange("(p t) c -> p t c", t=PACK))
            for n in range(count):
                raw["%s%d%d" % (m, j + n, o)] = rows[:, :, block(n)]

        def move_scales(queue):
            nc.vector.tensor_copy(x_rows[:], scale_table[:].indirect(picked[:]))
            for q in range(P // QUADRANT):
                queue.dma_start(
                    x_planes[QUADRANT * q : QUADRANT * q + 4].bitcast(I32),
                    x_rows[4 * PASSES * q : 4 * PASSES * (q + 1)].bitcast(I32),
                )

        scale_table = tile([P, T], U8, "scale_table")
        nc.gpsimd.memset(scale_table[QUADRANT : 2 * QUADRANT].bitcast(I32), 0)
        nc.gpsimd.memset(scale_table[2 * QUADRANT :].bitcast(I32), 0)
        x_planes = tile([P, PASSES, S], U8, "x_planes")
        nc.vector.memset(x_planes[:].rearrange("p o c -> p (o c)").bitcast(I32), 0)
        x_rows = tile([P, S], U8, "x_rows")

        picked = load_list("picked", offs)
        nc.sync.dma_start(scale_table[0:QUADRANT].bitcast(I32), x_scales.rearrange("o q c -> q o c").bitcast(I32))
        words = [load_words(o) for o in range(PASSES)]
        move_scales(nc.sync)
        load("a00")
        load("a01")
        first = load_list("first", pos1)
        second = load_list("second", pos2)
        third = load_list("third", pos3)
        for part in ("y00", "y01", "a10", "a11", "y10", "y11", "a20", "a21", "y20", "y21", "a30", "a31", "y30", "y31"):
            load(part)
        raw3 = tile([P, PACK, N], F32, "raw_w3")
        nc.sync.dma_start(raw3[:], w3.rearrange("(p t) c -> p t c", t=PACK))

        ident = keep.tile([P, P], F32, name="ident")
        make_identity(nc, ident[:])

        x_codes = [tile([P, S], U32, "x_codes%d" % o) for o in range(PASSES)]

        def pick(o, cols=slice(0, S)):
            entries = picked[:, cols.start // STRIPE : cols.stop // STRIPE]
            nc.vector.tensor_copy(x_codes[o][:, cols], words[o][:].indirect(entries))

        groups = {}
        home = {}

        def group(*parts, tag=None):
            values = tile([P, len(parts) * P, PACK], BF16, "grouped" + parts[0], tag)
            groups[parts[0]] = (values, parts)
            for place, part in enumerate(parts):
                home[part] = values[:, block(place), :]

        def cast(part, engine="V", share=slice(None)):
            if part not in home:
                group(part)
            copy = dict(V=nc.vector.tensor_copy, S=nc.scalar.copy)[engine]
            copy(
                home[part].rearrange("p (u l e) t -> p l t u e", u=2, e=2)[:, share],
                raw[part].rearrange("p t (l u e) -> p l t u e", u=2, e=2)[:, share],
            )

        def quantise(name, values, width, tag=None):
            codes = tile([P, width], U32, "codes" + name, tag)
            scales = tile([P, width], U8, "scales" + name)
            nc.vector.quantize_mx(codes[:].bitcast(FP8X4), scales[:], values)
            return codes, scales

        weights = {}

        def quant(name, tag=None):
            values, parts = groups[name]
            codes, scales = quantise(name, values[:].rearrange("p c t -> p (c t)"), len(parts) * P, tag)
            for place, part in enumerate(parts):
                weights[part] = (codes[:, block(place)].bitcast(FP8X4), scales[:, block(place)])

        accs = {}
        spans = [slice(0, 256), slice(256, 512), slice(256, 384), slice(384, 512)]

        def multiply(part, tag=None, half=None):
            o = int(part[2])
            key = part[:2] if half is None else part[:2] + str(half)
            cols = slice(0, S) if half is None else spans[half]
            if o == 0:
                accs[key] = bank(tag)
            nc.tensor.matmul_mx(
                out=accs[key][:, cols],
                lhsT=weights[part][0],
                lhsT_scale=weights[part][1],
                rhs=x_codes[o][:, cols].bitcast(FP8X4),
                rhs_scale=x_planes[:, o, cols],
                start=(o == 0),
                stop=(o == PASSES - 1),
            )

        rows = {}

        def bring(piece, engine="S", tag=None, half=None):
            if piece not in rows:
                rows[piece] = tile([P, S], F32, "rows" + piece, tag)
            copy = dict(V=nc.vector.tensor_copy, S=nc.scalar.copy)[engine]
            if half is None:
                copy(rows[piece][:], accs[piece][:])
            else:
                cols = spans[half]
                copy(rows[piece][:, cols], accs[piece + str(half)][:, cols])

        got = {}

        def fetch(kind, j, engine, half=None, tag=None, add=None, into=None):
            window = rows[kind[0] + str(j)]
            offsets = dict(a0=first, a1=second, y1=second, y2=third)[kind]
            name = "%s_%d" % (kind, j) + ("" if half is None else "h%d" % half)
            target = into if into is not None else tile([P, V if half is None else P], F32, name, tag)
            entries = offsets[:] if half is None else offsets[:, block(half, P // STRIPE)]
            if engine == "S":
                nc.scalar.activation(target[:], window[:].indirect(entries), ACT.Copy)
            elif add:
                nc.vector.tensor_tensor(target[:], window[:].indirect(entries), got[add, j, half], ALU.add)
            else:
                nc.vector.tensor_copy(target[:], window[:].indirect(entries))
            got[kind, j, half] = target[:]
            if half is None:
                for g in range(HALVES):
                    got[kind, j, g] = target[:, block(g)]

        def turn(target, kind, j, halves=range(HALVES), start=False, stop=False):
            for place, g in enumerate(halves):
                nc.tensor.matmul(
                    target[:, block(g if target.shape[1] > P else 0)], got[kind, j, g], ident[:],
                    start=start and place == 0, stop=stop and place == len(halves) - 1, is_transpose=True,
                )

        z_turned = tile([P, HALVES, 2, H // 2], BF16, "z_turned")

        def relu_of(name, sums, tag=None):
            one = tile([P, sums.shape[1]], F32, "one" + name, tag)
            nc.scalar.activation(one[:], sums, ACT.Relu)
            return one

        def join_sums(name, sums, one, tag=None):
            two = tile([P, sums.shape[1]], F32, "two" + name, tag)
            nc.vector.scalar_tensor_tensor(two[:], sums, 0.0, one[:], ALU.max, ALU.add)
            return two

        def close_sums(j, first_half, sums, two):
            halves = sums.shape[1] // P
            target = z_turned[:, first_half : first_half + halves, :, block(j, P // 2)]
            nc.vector.scalar_tensor_tensor(
                target.rearrange("p h u w -> p (h u) w"),
                sums.rearrange("p (r w) -> p r w", w=P // 2),
                0.0,
                two[:].rearrange("p (r w) -> p r w", w=P // 2),
                ALU.max,
                ALU.add,
            )

        def last_weights(tag=None, copy=nc.vector.tensor_copy):
            values = tile([P, N, PACK], BF16, "w3_grouped", tag)
            copy(values[:], raw3[:].rearrange("p t c -> p c t"))
            return values

        def turn_back(g, tag):
            back = bank(tag)
            for u in range(2):
                nc.tensor.transpose(back[:, block(u)], z_turned[:, g, u, :].bitcast(F32), ident[:])
            z_grouped = tile([P, P, 2], F32, "z_grouped%d" % g)
            nc.scalar.copy(z_grouped[:], back[:, 0 : 2 * P].rearrange("p (u v) -> p v u", u=2))
            return z_grouped[:].rearrange("p v u -> p (v u)").bitcast(BF16)

        def finish(g, packed, tag):
            z_codes, z_scales = quantise("z%d" % g, packed, P)
            acc = bank(tag)
            nc.tensor.matmul_mx(
                out=acc[:, 0:P],
                lhsT=w3_codes[:].bitcast(FP8X4),
                lhsT_scale=w3_scales[:],
                rhs=z_codes[:].bitcast(FP8X4),
                rhs_scale=z_scales[:],
                start=True,
                stop=True,
            )
            result = tile([P, P], F32, "result%d" % g)
            nc.scalar.activation(result[:], acc[:, 0:P], ACT.Relu)
            nc.sync.dma_start(out[:, block(g)], result[:])

        def part(name, tag=None, filler=None):
            cast(name)
            if filler:
                filler()
            quant(name)
            multiply(name, tag)
        def f(*a, **k):
            return lambda: fetch(*a, **k)
        def lone(tag, kinds, j, halves=range(HALVES)):
            o = bank(tag)[:, 0 : len(halves) * P]
            for n, kind in enumerate(kinds):
                turn(o, kind, j, halves, start=n == 0, stop=n == len(kinds) - 1)
            return o
        def other_sums(j, tag, fused):
            both = bank(tag)
            turn(both[:, 0:V], "a0", j, start=True)
            turn(both[:, 0:V], "y2", j)
            turn(both[:, V:], "a0", j, [g for g in range(HALVES) if g not in fused])
            turn(both[:, V:], "y1", j, stop=True)
            return both[:, 0:V], both[:, V:]
        pick(0)
        pick(1)
        cast("a00")
        cast("a01", "V", slice(0, 16))
        cast("a01", "S", slice(16, 32))
        quant("a00")
        quant("a01")
        for name in ("a00", "a01"):
            for g in range(2):
                multiply(name, ("b0", "b3")[g], g)
        part("y00", "b1")
        bring("a0", "S", "rawy00", half=0)
        cast("y01")
        bring("a0", "V", half=1)
        quant("y01")
        multiply("y01")
        fetch("a0", 0, "S")
        bring("y0")
        part("a10", "b2", f("a1", 0, "V", 0, "rawy01"))
        part("a11", None, f("a1", 0, "V", 1, "rawa10"))
        fetch("y2", 0, "S")
        o0 = lone("b4", ["y2", "a1"], 0)
        bring("a1")
        fetch("y1", 0, "S", 1, tag="codesa11")
        fetch("a0", 1, "S")
        part("y10", "b0", f("y1", 0, "V", 0, "rawa11", "a0"))
        part("y11")
        s0 = other_sums(0, "b2", [0])
        bring("y1")
        one0 = relu_of("0", o0, "codesy11")
        fetch("y2", 1, "S")
        part("a20", "b3", f("a1", 1, "V", 0, "rawy11"))
        part("a21", None, f("a1", 1, "V", 1, "rawa20"))
        o1 = lone("b4", ["y2", "a1"], 1)
        bring("a2")
        fetch("y1", 1, "S", tag="codesa21")
        fetch("a0", 2, "S")
        cast("y20")
        two0 = join_sums("0", s0[0], one0, "rawa21")
        cast("y21")
        quant("y20")
        multiply("y20", "b1")
        quant("y21")
        multiply("y21")
        close_sums(0, 0, s0[1], two0)
        s1 = other_sums(1, "b2", [])
        bring("y2")
        one1 = relu_of("1", o1, "codesy21")
        fetch("y2", 2, "S")
        part("a30", "b3", f("a1", 2, "V", 0, "rawy21"))
        part("a31", None, f("a1", 2, "V", 1, "rawa30"))
        o2 = lone("b4", ["y2", "a1"], 2)
        bring("a3")
        fetch("y1", 2, "S", 1, tag="codesa31")
        fetch("a0", 3, "S")
        cast("y30")
        cast("y31")
        quant("y30")
        quant("y31")
        fetch("y1", 2, "V", 0, add="a0", tag="rawy31")
        two1 = join_sums("1", s1[0], one1, "rawy30")
        fetch("a1", 3, "V", 1)
        for name in ("y30", "y31"):
            for g in range(2):
                multiply(name, ("b0", "b1")[g], g)
        s2 = other_sums(2, "b3", [0])
        bring("y3", "S", half=0)
        bring("y3", "V", half=1)
        one2 = relu_of("2", o2, "codesy31")
        close_sums(1, 0, s1[1], two1)
        fetch("a1", 3, "V", 0, tag="scalesy31")
        fetch("y2", 3, "S", 0)
        fetch("y2", 3, "V", 1)
        fetch("y1", 3, "S", 1)
        two2 = join_sums("2", s2[0], one2)
        fetch("y1", 3, "V", 0, add="a0")
        p = [bank(("b5", "b6")[g])[:, 0:P] for g in range(2)]
        r = [bank(("b4", "b7")[g])[:, 0:P] for g in range(2)]
        l31 = bank("b2")[:, 0:P]
        for g in range(2):
            turn(p[g], "a0", 3, [g], start=True)
        turn(r[1], "a1", 3, [1], start=True)
        turn(l31, "a0", 3, [1], start=True)
        turn(r[0], "a1", 3, [0], start=True)
        for g in range(2):
            turn(p[g], "y2", 3, [g], stop=True)
        for g in range(2):
            turn(r[g], "y2", 3, [g], stop=True)
        l30 = lone("b0", ["y1"], 3, [0])
        turn(l31, "y1", 3, [1], stop=True)
        ones = [relu_of("3h%d" % g, p[g]) for g in range(2)]
        close_sums(2, 0, s2[1], two2)
        twos = [join_sums("3h%d" % g, r[g], ones[g]) for g in range(2)]
        close_sums(3, 0, l30, twos[0])
        close_sums(3, 1, l31, twos[1])
        w3_values = last_weights("two3h0")
        w3_codes, w3_scales = quantise("w3", w3_values[:].rearrange("p c t -> p (c t)"), N)
        packed = [turn_back(g, ("b1", "b3")[g]) for g in range(2)]
        for g in range(2):
            finish(g, packed[g], ("b5", "b6")[g])
